import numpy as np
import ml_dtypes


def mxq(x, axis, fmt="e4m3"):
    dtype, down = {"e4m3": (ml_dtypes.float8_e4m3fn, 7), "e5m2": (ml_dtypes.float8_e5m2, 14)}[fmt]
    v = np.moveaxis(np.asarray(x, np.float32).astype(ml_dtypes.bfloat16).astype(np.float64), axis, -1)
    blocks = v.reshape(v.shape[:-1] + (-1, 32))
    amax = np.abs(blocks).max(-1, keepdims=True)
    byte = np.maximum(np.where(amax > 0, np.frexp(amax)[1] - 1 + 127, 0) - down, 1)
    scale = np.exp2(byte - 127.0)
    codes = (blocks / scale).astype(np.float32).astype(dtype).astype(np.float64)
    return np.moveaxis((codes * scale).reshape(v.shape), -1, axis)


WIDE = False


def mx_kscale(k):
    if not WIDE:
        return np.ones(k)
    levels = np.array([10, -10, 5, -5, 0])
    if k % 512:
        return np.exp2(np.random.permutation(np.resize(levels, k // 32))).repeat(32)
    a = np.empty((k // 512, 16))
    for p in range(k // 512):
        a[p, :8] = np.random.permutation(np.resize(levels, 8))
        for g in range(8):
            far = levels[np.abs(levels - a[p, g]) >= 10]
            a[p, g + 8] = far[np.random.randint(len(far))]
    return np.exp2(a.ravel()).repeat(32)


BF16 = ml_dtypes.bfloat16


def bf(x):
    return np.asarray(x, np.float32).astype(BF16)


def f64(x):
    return np.asarray(x).astype(np.float64)


E2M1 = np.array([0.0, 0.5, 1.0, 1.5, 2.0, 3.0, 4.0, 6.0, -0.0, -0.5, -1.0, -1.5, -2.0, -3.0, -4.0, -6.0])


def pack_weight(w, fmt):
    k, n = w.shape
    w = f64(bf(w)).reshape(k // 32, 32, n)
    amax = np.abs(w).max(1)
    if fmt == "e4m3":
        byte = np.frexp(amax)[1] - 1 + 127 - 7
    else:
        mant, ex = np.frexp(amax / 6.0)
        byte = np.where(mant > 0.5, ex, ex - 1) + 127
    byte = np.clip(np.where(amax > 0, byte, 1), 1, 254)
    scaled = (w * np.exp2(127.0 - byte)[:, None, :]).reshape(k, n).astype(np.float32)
    by_word = np.ascontiguousarray(scaled.reshape(k // 512, 128, 4, n).transpose(0, 1, 3, 2))
    if fmt == "e4m3":
        words = by_word.astype(ml_dtypes.float8_e4m3fn).view(np.uint8)
    else:
        c = by_word.astype(ml_dtypes.float4_e2m1fn).view(np.uint8) & 0xF
        words = c[..., 0::2] | (c[..., 1::2] << 4)
    return np.ascontiguousarray(words), np.ascontiguousarray(byte.astype(np.uint8).reshape(k // 512, 16, n))


def unpack_weight(words, scales, fmt):
    g, p, n, _ = words.shape
    if fmt == "e4m3":
        vals = np.ascontiguousarray(words).view(ml_dtypes.float8_e4m3fn).astype(np.float64)
    else:
        nib = np.empty((g, p, n, 4), np.uint8)
        nib[..., 0::2] = words & 0xF
        nib[..., 1::2] = words >> 4
        vals = E2M1[nib]
    vals = vals * np.repeat(np.exp2(scales.astype(np.float64) - 127.0), 8, axis=1)[..., None]
    return vals.transpose(0, 1, 3, 2).reshape(g * 512, n)
def pack4(w):
    words, scales = pack_weight(w, "e2m1")
    return words.reshape(words.shape[0], 128, -1), scales


def unpack4(words, scales):
    return unpack_weight(words.reshape(words.shape[0], 128, -1, 2), scales, "e2m1")


def planes(Y):
    n, m = Y.shape
    b = f64(bf(Y)).reshape(n // 32, 32, m)
    amax = np.abs(b).max(1)
    byte = np.clip(np.where(amax > 0, np.frexp(amax)[1] - 1 + 127 - 7, 1), 1, 254)
    codes = (b * np.exp2(127.0 - byte)[:, None, :]).reshape(n, m).astype(np.float32).astype(ml_dtypes.float8_e4m3fn).view(np.uint8)
    words = codes.reshape(n // 512, 128, 4, m).transpose(0, 1, 3, 2)
    return np.ascontiguousarray(words), np.ascontiguousarray(byte.astype(np.uint8).reshape(n // 512, 16, m))


HEADS, TOKENS, D, VOCAB = 4, 512, 1024, 1024
CAP = 2.0

def setup_inputs():
    s = mx_kscale(D)
    x = np.random.randn(TOKENS, D) * s[None, :]
    w = np.random.randn(HEADS, D, D) / np.sqrt(D) / s[None, :, None]
    w_words, w_scales = pack4(w.reshape(HEADS * D, D))
    branch_gain = (1.0 + 0.1 * np.random.randn(HEADS, D)) * s[None, :]
    unembed = 0.4 * np.random.randn(D, VOCAB) / np.sqrt(D) / s[:, None]
    token_weight = np.exp(0.8 * np.random.randn(HEADS, VOCAB))
    return {"x": bf(x), "w_words": w_words, "w_scales": w_scales, "branch_gain": bf(branch_gain),
            "unembed": bf(unembed), "token_weight": bf(token_weight)}

def reference(x, w_words, w_scales, branch_gain, unembed, token_weight):
    X, gain, U, weight = f64(x), f64(branch_gain), f64(unembed), f64(token_weight)
    W = unpack4(w_words, w_scales).reshape(HEADS, D, D)
    Z = mxq(X, 1) @ W
    H = X + gain[:, None, :] * (Z / (1.0 + np.exp(-Z)))
    L = mxq(H, 2) @ mxq(U, 0)
    y = weight[:, None, :] * np.exp(CAP * np.tanh(L))
    Y = y.reshape(HEADS * TOKENS, VOCAB).T
    words, scales = planes(Y)
    return y, words, scales

@@ -1,0 +1,385 @@
+from contextlib import ExitStack
+
+import concourse.mybir as mybir
+from concourse.masks import make_identity
+
+HEADS, TOKENS, D, VOCAB = 4, 512, 1024, 1024
+CAP = 2.0
+FLOPS = 2 * HEADS * TOKENS * D * (D + VOCAB)
+
+F32 = mybir.dt.float32
+BF16 = mybir.dt.bfloat16
+I32 = mybir.dt.int32
+U32 = mybir.dt.uint32
+U8 = mybir.dt.uint8
+FP8X4 = mybir.dt.float8_e4m3fn_x4
+FP4X4 = mybir.dt.float4_e2m1fn_x4
+ACT = mybir.ActivationFunctionType
+ALU = mybir.AluOpType
+
+P = 128
+PACK = 4
+PASS = P * PACK
+GROUPS = D // PASS
+TOK_TILES = TOKENS // P
+UNITS = HEADS * GROUPS
+LN_LOW, LN_HIGH = 2.0**-63, 2.0**63
+SCALAR_EVAC_UNITS = (0, 1, 2, 3, 7)
+
+
+def tile_draft_heads_shared_unembedding_k7_kernel(
+    tc, x, w_words, w_scales, branch_gain, unembed, token_weight, out_0, out_1, out_2
+):
+    nc = tc.nc
+    with ExitStack() as ctx:
+        keep = ctx.enter_context(tc.tile_pool(name="keep", bufs=1))
+        psum = ctx.enter_context(tc.psum_pool(name="psum", bufs=4))
+        ctx.enter_context(tc.manual_schedule())
+        with tc.tile_pool(name="early", bufs=1) as early:
+
+            ident32 = keep.tile([P, P], F32, name="ident32")
+            ident16 = keep.tile([P, P], BF16, name="ident16")
+            gain = keep.tile([P, PACK, UNITS], F32, name="gain")
+            ln_w = keep.tile([P, PACK, UNITS], F32, name="ln_w")
+            x_res = keep.tile([P, GROUPS, PACK, TOKENS], BF16, name="x_res")
+            x_codes = keep.tile([P, GROUPS, TOKENS], U32, name="x_codes", align_bytes=64)
+            x_scale = keep.tile([P, GROUPS, TOKENS], U8, name="x_scale", align_bytes=64)
+            w_codes = keep.tile([P, HEADS, GROUPS, 2 * D], U8, name="w_codes", align_bytes=64)
+            w_scale = keep.tile([P, HEADS, GROUPS, D], U8, name="w_scale", align_bytes=64)
+            u_codes = keep.tile([P, GROUPS, VOCAB], U32, name="u_codes", align_bytes=64)
+            u_scale = keep.tile([P, GROUPS, VOCAB], U8, name="u_scale", align_bytes=64)
+
+            vec = early.tile([P, PASS], BF16, name="vec")
+            vec_sorted = early.tile([P, PACK, P], BF16, name="vec_sorted")
+            w_parts = early.tile([P, 2, PACK, UNITS], F32, name="w_parts")
+            w_inverse = early.tile([P, PACK, UNITS], F32, name="w_inverse")
+            ln_parts = early.tile([P, 2, PACK, UNITS], F32, name="ln_parts")
+            x_raw = early.tile([P, TOK_TILES, D], BF16, name="x_raw")
+            x_sorted = early.tile([P, TOK_TILES, D], BF16, name="x_sorted")
+            x_packed = early.tile([P, GROUPS, TOKENS, PACK], BF16, name="x_packed", align_bytes=64)
+            w_codes_raw = early.tile([P, HEADS, GROUPS, 2 * D], U8, name="w_codes_raw")
+            w_scale_raw = early.tile([P, HEADS * GROUPS, D], U8, name="w_scale_raw")
+            u_raw = early.tile([P, GROUPS, PACK, VOCAB], BF16, name="u_raw")
+
+            def load_x(first):
+                nc.sync.dma_start(
+                    out=x_raw[:, first : first + 2, :],
+                    in_=x[first * P : (first + 2) * P, :].rearrange("(c p) d -> p c d", p=P),
+                )
+
+            def load_w(h):
+                nc.sync.dma_start(
+                    out=w_codes_raw[:, h, :, :].bitcast(I32),
+                    in_=w_words[GROUPS * h : GROUPS * (h + 1), :, :].rearrange("a p n -> p a n").bitcast(I32),
+                )
+
+            def load_w_scale(first, last):
+                rows = slice(GROUPS * first, GROUPS * last)
+                nc.vector.memset(w_scale_raw[:, rows, :].rearrange("p a n -> p (a n)").bitcast(I32), 0)
+                for q in range(4):
+                    nc.sync.dma_start(
+                        out=w_scale_raw[32 * q : 32 * q + 4, rows, :].bitcast(I32),
+                        in_=w_scales[rows, 4 * q : 4 * q + 4, :].rearrange("a r n -> r a n").bitcast(I32),
+                    )
+
+            nc.gpsimd.memset(vec[:].bitcast(I32), 0)
+            load_x(0)
+            nc.sync.dma_start(out=vec[0:UNITS, :], in_=token_weight.rearrange("h (g v) -> (h g) v", g=GROUPS))
+            nc.sync.dma_start(out=vec[64 : 64 + UNITS, :], in_=branch_gain.rearrange("h (g v) -> (h g) v", g=GROUPS))
+            load_x(2)
+            make_identity(nc, ident16[:])
+            make_identity(nc, ident32[:])
+            load_w(0)
+            load_w_scale(0, 1)
+            load_w(1)
+            load_w_scale(1, HEADS)
+            load_w(2)
+            load_w(3)
+            for kg in range(GROUPS):
+                rows = unembed[kg * PASS : (kg + 1) * PASS, :].rearrange("(q t r) v -> t q r v", t=PACK, r=8)
+                for t in range(PACK):
+                    nc.sync.dma_start(out=u_raw[:, kg, t, :], in_=rows[t])
+
+            nc.vector.tensor_copy(
+                out=vec_sorted[0:64, :, :], in_=vec[0:64, :].rearrange("a (p t) -> a t p", t=PACK)
+            )
+            nc.vector.tensor_copy(
+                out=vec_sorted[64:128, :, :].rearrange("a t (q r) -> a t q r", r=8),
+                in_=vec[64:128, :].rearrange("a (q t r) -> a t q r", t=PACK, r=8),
+            )
+            vec_t = psum.tile([P, PACK, P], BF16, name="vec_t", tag="tr")
+            for t in range(PACK):
+                nc.tensor.transpose(vec_t[:, t, :], vec_sorted[:, t, :], ident16[:])
+
+            def sort_x(c):
+                nc.vector.tensor_copy(
+                    out=x_sorted[:, c, :].bitcast(F32).rearrange("a (g t q w) -> a g t q w", g=GROUPS, t=PACK, w=4),
+                    in_=x_raw[:, c, :].bitcast(F32).rearrange("a (g q t w) -> a g t q w", g=GROUPS, t=PACK, w=4),
+                )
+
+            nc.vector.tensor_scalar(
+                out=w_parts[:, 0, :, :], in0=vec_t[:, :, 0:UNITS], scalar1=LN_LOW, scalar2=LN_HIGH,
+                op0=ALU.max, op1=ALU.min,
+            )
+            sort_x(0)
+            nc.vector.reciprocal(out=w_inverse[:], in_=w_parts[:, 0, :, :])
+            sort_x(1)
+            nc.vector.tensor_tensor(out=w_parts[:, 1, :, :], in0=vec_t[:, :, 0:UNITS], in1=w_inverse[:], op=ALU.mult)
+            nc.vector.tensor_copy(out=gain[:], in_=vec_t[:, :, 64 : 64 + UNITS])
+            nc.scalar.activation(out=ln_parts[:], in_=w_parts[:], func=ACT.Ln)
+            sort_x(2)
+            sort_x(3)
+
+            x_packed_words = x_packed[:].rearrange("p g n t -> p (g n t)").bitcast(F32).rearrange(
+                "p (g n u) -> p g n u", g=GROUPS, u=2
+            )
+            for c in range(TOK_TILES):
+                words = x_raw[:, c, :].bitcast(F32)
+                bank = psum.tile([P, GROUPS, 2, P], F32, name="x_words_t", tag="mm")
+                for g in range(GROUPS):
+                    for u in range(2):
+                        nc.tensor.transpose(bank[:, g, u, :], words[:, 256 * g + u : 256 * (g + 1) : 2], ident32[:])
+                nc.scalar.copy(
+                    out=x_packed_words[:, :, c * P : (c + 1) * P, :], in_=bank[:].rearrange("p g u n -> p g n u")
+                )
+
+            def sort_w(h):
+                nc.vector.tensor_copy(
+                    out=w_codes[:, h, :, :].rearrange("p a n -> p (a n)").bitcast(I32).rearrange(
+                        "p (b t q w) -> p b t q w", t=PACK, q=16, w=4
+                    ),
+                    in_=w_codes_raw[:, h, :, :].rearrange("p a n -> p (a n)").bitcast(I32).rearrange(
+                        "p (b q t w) -> p b t q w", t=PACK, q=16, w=4
+                    ),
+                )
+                nc.vector.tensor_copy(
+                    out=w_scale[:, h, :, :].rearrange("p a n -> p (a n)").bitcast(I32).rearrange(
+                        "p (b t q w) -> p b t q w", t=PACK, q=16, w=2
+                    ),
+                    in_=w_scale_raw[:, GROUPS * h : GROUPS * (h + 1), :].rearrange("p a n -> p (a n)").bitcast(I32).rearrange(
+                        "p (b q t w) -> p b t q w", t=PACK, q=16, w=2
+                    ),
+                )
+
+            sort_w(0)
+            for g in range(GROUPS):
+                nc.vector.quantize_mx(
+                    out=x_codes[:, g, :].bitcast(FP8X4),
+                    scales=x_scale[:, g, :],
+                    in_=x_packed[:, g, :, :].rearrange("p n t -> p (n t)"),
+                )
+            nc.vector.tensor_tensor(out=ln_w[:], in0=ln_parts[:, 0, :, :], in1=ln_parts[:, 1, :, :], op=ALU.add)
+
+            for g in range(GROUPS):
+                for half in range(2):
+                    bank = psum.tile([P, 2, TOKENS], BF16, name="x_res_t", tag="tr")
+                    for tt in range(2):
+                        col = g * PASS + (2 * half + tt) * P
+                        for c in range(TOK_TILES):
+                            nc.tensor.transpose(
+                                bank[:, tt, c * P : (c + 1) * P], x_sorted[:, c, col : col + P], ident16[:]
+                            )
+                    nc.scalar.copy(out=x_res[:, g, 2 * half : 2 * half + 2, :], in_=bank[:])
+
+            silu = {}
+
+            def project(u):
+                h, g = divmod(u, GROUPS)
+                silu[u] = keep.tile([P, PACK, TOKENS], F32, name="silu", tag="silu", bufs=6)
+                for t in range(PACK):
+                    col = g * PASS + t * P
+                    bank = psum.tile([P, TOKENS], F32, name="z", tag="mm")
+                    for kg in range(GROUPS):
+                        nc.tensor.matmul_mx(
+                            out=bank[:],
+                            lhsT=w_codes[:, h, kg, 2 * col : 2 * (col + P)].bitcast(FP4X4),
+                            lhsT_scale=w_scale[:, h, kg, col : col + P],
+                            rhs=x_codes[:, kg, :].bitcast(FP8X4),
+                            rhs_scale=x_scale[:, kg, :],
+                            start=(kg == 0),
+                            stop=(kg == GROUPS - 1),
+                        )
+                    nc.scalar.activation(out=silu[u][:, t, :], in_=bank[:], func=ACT.Silu)
+
+            hidden, hidden_packed, h_codes, h_scale = {}, {}, {}, {}
+
+            def residual(u):
+                g = u % GROUPS
+                hidden[u] = keep.tile([P, PACK, TOKENS], BF16, name="hidden", tag="hidden", bufs=2)
+                for t in range(PACK):
+                    nc.vector.scalar_tensor_tensor(
+                        out=hidden[u][:, t, :], in0=silu[u][:, t, :], scalar=gain[:, t, u : u + 1],
+                        in1=x_res[:, g, t, :], op0=ALU.mult, op1=ALU.add,
+                    )
+
+            def interleave(dst, src):
+                nc.vector.tensor_copy(
+                    out=dst.rearrange("p (c i) t -> p c t i", i=4), in_=src.rearrange("p t (c i) -> p c t i", i=4)
+                )
+
+            def pack_hidden(u):
+                hidden_packed[u] = keep.tile(
+                    [P, TOKENS, PACK], BF16, name="hidden_packed", tag="hidden_packed", bufs=2, align_bytes=64
+                )
+                interleave(hidden_packed[u][:], hidden[u][:])
+
+            def quantize_hidden(u):
+                h_codes[u] = keep.tile([P, TOKENS], U32, name="h_codes", tag="h_codes", bufs=6, align_bytes=64)
+                h_scale[u] = keep.tile([P, TOKENS], U8, name="h_scale", tag="h_scale", bufs=6, align_bytes=64)
+                nc.vector.quantize_mx(
+                    out=h_codes[u][:].bitcast(FP8X4),
+                    scales=h_scale[u][:],
+                    in_=hidden_packed[u][:].rearrange("p n t -> p (n t)"),
+                )
+
+            u_packed = {}
+
+            def pack_u(kg, g):
+                u_packed[kg, g] = early.tile(
+                    [P, PACK, P, PACK], BF16, name="u_packed", tag="u_packed", bufs=2, align_bytes=64
+                )
+                nc.vector.tensor_copy(
+                    out=u_packed[kg, g][:].rearrange("p t m j -> p m t j"),
+                    in_=u_raw[:, kg, :, g * PASS : (g + 1) * PASS].rearrange("p j (m t) -> p m t j", t=PACK),
+                )
+
+            def quantize_u(kg, g):
+                nc.vector.quantize_mx(
+                    out=u_codes[:, kg, g * PASS : (g + 1) * PASS].bitcast(FP8X4),
+                    scales=u_scale[:, kg, g * PASS : (g + 1) * PASS],
+                    in_=u_packed[kg, g][:].rearrange("p t m j -> p (t m j)"),
+                )
+
+            project(0)
+            sort_w(1)
+            project(1)
+            sort_w(2)
+            residual(0)
+            sort_w(3)
+            pack_hidden(0)
+            for u in range(2, 6):
+                project(u)
+            residual(1)
+            quantize_hidden(0)
+            pack_hidden(1)
+            for u in range(6, UNITS):
+                project(u)
+            pack_u(0, 0)
+            quantize_hidden(1)
+            pack_u(1, 0)
+            quantize_u(0, 0)
+            pack_u(0, 1)
+            quantize_u(1, 0)
+            pack_u(1, 1)
+            quantize_u(0, 1)
+            residual(2)
+            quantize_u(1, 1)
+        late = ctx.enter_context(tc.tile_pool(name="late", bufs=1))
+        y_scale = late.tile([P, GROUPS, HEADS * TOKENS], U8, name="y_scale", align_bytes=64)
+
+        y_t, y_packed, y_banks, y_rows, logits = {}, {}, {}, {}, {}
+
+        def unembed_matmuls(u):
+            h, g = divmod(u, GROUPS)
+            for t in range(PACK):
+                col = g * PASS + t * P
+                logits[u, t] = psum.tile([P, TOKENS], F32, name="logits", tag="mm")
+                for kg in range(GROUPS):
+                    nc.tensor.matmul_mx(
+                        out=logits[u, t][:],
+                        lhsT=u_codes[:, kg, col : col + P].bitcast(FP8X4),
+                        lhsT_scale=u_scale[:, kg, col : col + P],
+                        rhs=h_codes[GROUPS * h + kg][:].bitcast(FP8X4),
+                        rhs_scale=h_scale[GROUPS * h + kg][:],
+                        start=(kg == 0),
+                        stop=(kg == GROUPS - 1),
+                    )
+
+        def soft_cap(u):
+            y_t[u] = keep.tile([P, PACK, TOKENS], F32, name="y_t", tag="y_t", bufs=3)
+            for t in range(PACK):
+                nc.scalar.activation(out=y_t[u][:, t, :], in_=logits[u, t][:], func=ACT.Tanh)
+
+        def weigh(u):
+            for t in range(PACK):
+                nc.scalar.activation(
+                    out=y_t[u][:, t, :], in_=y_t[u][:, t, :], func=ACT.Exp, bias=ln_w[:, t, u : u + 1], scale=CAP
+                )
+
+        def transpose_y(u):
+            for c in range(TOK_TILES):
+                y_banks[u, c] = psum.tile([P, PACK, P], F32, name="y_bank", tag="tr")
+                for t in range(PACK):
+                    nc.tensor.transpose(y_banks[u, c][:, t, :], y_t[u][:, t, c * P : (c + 1) * P], ident32[:])
+
+        def store_rows(u):
+            h, g = divmod(u, GROUPS)
+            copy = nc.scalar.copy if u in SCALAR_EVAC_UNITS else nc.vector.tensor_copy
+            y_rows[u] = late.tile([P, TOK_TILES, PASS], F32, name="y_rows", tag="y_rows", bufs=3)
+            dest = out_0[h, :, g * PASS : (g + 1) * PASS].rearrange("(c p) v -> p c v", p=P)
+            for c in range(TOK_TILES):
+                copy(
+                    out=y_rows[u][:, c, :].rearrange("a (p t) -> a p t", t=PACK),
+                    in_=y_banks[u, c][:].rearrange("a t p -> a p t"),
+                )
+                if u == UNITS - 1:
+                    nc.sync.dma_start(out=dest[:, c, :], in_=y_rows[u][:, c, :])
+            if u < UNITS - 1:
+                nc.sync.dma_start(out=dest, in_=y_rows[u][:])
+
+        def pack_y(u):
+            y_packed[u] = late.tile([P, TOKENS, PACK], BF16, name="y_packed", tag="y_packed", bufs=2, align_bytes=64)
+            interleave(y_packed[u][:], y_t[u][:])
+
+        def quantize_y(u):
+            h, g = divmod(u, GROUPS)
+            y_codes = late.tile([P, TOKENS], U32, name="y_codes", tag="y_codes", bufs=3, align_bytes=64)
+            nc.vector.quantize_mx(
+                out=y_codes[:].bitcast(FP8X4),
+                scales=y_scale[:, g, h * TOKENS : (h + 1) * TOKENS],
+                in_=y_packed[u][:].rearrange("p n t -> p (n t)"),
+            )
+            nc.sync.dma_start(
+                out=out_1[g].rearrange("p m t -> p (m t)")[:, PACK * h * TOKENS : PACK * (h + 1) * TOKENS].bitcast(I32),
+                in_=y_codes[:].bitcast(I32),
+            )
+
+        def store_scales(first, last):
+            cols = slice(first * TOKENS, last * TOKENS)
+            for q in range(4):
+                nc.sync.dma_start(
+                    out=out_2[:, 4 * q : 4 * q + 4, cols].rearrange("g r m -> r g m").bitcast(I32),
+                    in_=y_scale[32 * q : 32 * q + 4, :, cols].bitcast(I32),
+                )
+
+        unembed_matmuls(0)
+        soft_cap(0)
+        unembed_matmuls(1)
+        weigh(0)
+        pack_hidden(2)
+        residual(3)
+        quantize_hidden(2)
+        pack_hidden(3)
+        for u in range(UNITS):
+            transpose_y(u)
+            pack_y(u)
+            if u + 3 < UNITS:
+                quantize_hidden(u + 3)
+            if u + 1 < UNITS:
+                soft_cap(u + 1)
+            if u + 2 < UNITS:
+                unembed_matmuls(u + 2)
+            if u == UNITS - 1:
+                quantize_y(u)
+                store_scales(HEADS - 1, HEADS)
+            store_rows(u)
+            if u + 1 < UNITS:
+                weigh(u + 1)
+            if u + 4 < UNITS:
+                residual(u + 4)
+            if u < UNITS - 1:
+                quantize_y(u)
+            if u + 4 < UNITS:
+                pack_hidden(u + 4)
+            if u == UNITS - 3:
+                store_scales(0, HEADS - 1)

@@ -24,7 +24,9 @@ GROUPS = D // PASS
 TOK_TILES = TOKENS // P
 UNITS = HEADS * GROUPS
 LN_LOW, LN_HIGH = 2.0**-63, 2.0**63
-SCALAR_EVAC_UNITS = (0, 1, 2, 3, 7)
+SCALAR_EVACS = 11
+STEPS = UNITS * PACK
+HALF = TOKENS // 2
 
 
 def tile_draft_heads_shared_unembedding_k7_kernel(
@@ -55,17 +57,15 @@ def tile_draft_heads_shared_unembedding_k7_kernel(
             w_inverse = early.tile([P, PACK, UNITS], F32, name="w_inverse")
             ln_parts = early.tile([P, 2, PACK, UNITS], F32, name="ln_parts")
             x_raw = early.tile([P, TOK_TILES, D], BF16, name="x_raw")
+            x_words = early.tile([P, TOK_TILES, GROUPS, 2, P], F32, name="x_words")
             x_sorted = early.tile([P, TOK_TILES, D], BF16, name="x_sorted")
             x_packed = early.tile([P, GROUPS, TOKENS, PACK], BF16, name="x_packed", align_bytes=64)
             w_codes_raw = early.tile([P, HEADS, GROUPS, 2 * D], U8, name="w_codes_raw")
             w_scale_raw = early.tile([P, HEADS * GROUPS, D], U8, name="w_scale_raw")
             u_raw = early.tile([P, GROUPS, PACK, VOCAB], BF16, name="u_raw")
 
-            def load_x(first):
-                nc.sync.dma_start(
-                    out=x_raw[:, first : first + 2, :],
-                    in_=x[first * P : (first + 2) * P, :].rearrange("(c p) d -> p c d", p=P),
-                )
+            def load_x(c):
+                nc.sync.dma_start(out=x_raw[:, c, :], in_=x[c * P : (c + 1) * P, :])
 
             def load_w(h):
                 nc.sync.dma_start(
@@ -82,23 +82,59 @@ def tile_draft_heads_shared_unembedding_k7_kernel(
                         in_=w_scales[rows, 4 * q : 4 * q + 4, :].rearrange("a r n -> r a n").bitcast(I32),
                     )
 
+            def load_u(kg):
+                rows = unembed[kg * PASS : (kg + 1) * PASS, :].rearrange("(q t r) v -> t q r v", t=PACK, r=8)
+                for t in range(PACK):
+                    nc.sync.dma_start(out=u_raw[:, kg, t, :], in_=rows[t])
+
             nc.gpsimd.memset(vec[:].bitcast(I32), 0)
-            load_x(0)
             nc.sync.dma_start(out=vec[0:UNITS, :], in_=token_weight.rearrange("h (g v) -> (h g) v", g=GROUPS))
             nc.sync.dma_start(out=vec[64 : 64 + UNITS, :], in_=branch_gain.rearrange("h (g v) -> (h g) v", g=GROUPS))
+            load_x(0)
+            load_x(1)
             load_x(2)
+            load_x(3)
             make_identity(nc, ident16[:])
             make_identity(nc, ident32[:])
             load_w(0)
             load_w_scale(0, 1)
-            load_w(1)
+            load_u(0)
             load_w_scale(1, HEADS)
+            load_w(1)
+            load_u(1)
             load_w(2)
             load_w(3)
-            for kg in range(GROUPS):
-                rows = unembed[kg * PASS : (kg + 1) * PASS, :].rearrange("(q t r) v -> t q r v", t=PACK, r=8)
-                for t in range(PACK):
-                    nc.sync.dma_start(out=u_raw[:, kg, t, :], in_=rows[t])
+
+            x_packed_words = x_packed[:].rearrange("p g n t -> p (g n t)").bitcast(F32).rearrange(
+                "p (g n u) -> p g n u", g=GROUPS, u=2
+            )
+            word_banks = {}
+
+            def sort_x(c, copy):
+                copy(
+                    out=x_sorted[:, c, :].bitcast(F32).rearrange("a (g t q w) -> a g t q w", t=PACK, q=16, w=4),
+                    in_=x_raw[:, c, :].bitcast(F32).rearrange("a (g q t w) -> a g t q w", t=PACK, q=16, w=4),
+                )
+
+            def transpose_x_words(c):
+                nc.vector.tensor_copy(
+                    out=x_words[:, c, :, :, :],
+                    in_=x_raw[:, c, :].bitcast(F32).rearrange("a (g p u) -> a g u p", g=GROUPS, u=2),
+                )
+                for g in range(GROUPS):
+                    if c % 2 == 0:
+                        word_banks[c // 2, g] = psum.tile([P, 2, 2, P], F32, name="x_words_t", tag="mm")
+                    for u in range(2):
+                        nc.tensor.transpose(word_banks[c // 2, g][:, c % 2, u, :], x_words[:, c, g, u, :], ident32[:])
+
+            def pack_x(pair):
+                for g in range(GROUPS):
+                    nc.scalar.copy(
+                        out=x_packed_words[:, g, 2 * pair * P : 2 * (pair + 1) * P, :].rearrange(
+                            "p (c n) u -> p c n u", c=2
+                        ),
+                        in_=word_banks[pair, g][:].rearrange("p c u n -> p c n u"),
+                    )
 
             nc.vector.tensor_copy(
                 out=vec_sorted[0:64, :, :], in_=vec[0:64, :].rearrange("a (p t) -> a t p", t=PACK)
@@ -110,40 +146,24 @@ def tile_draft_heads_shared_unembedding_k7_kernel(
             vec_t = psum.tile([P, PACK, P], BF16, name="vec_t", tag="tr")
             for t in range(PACK):
                 nc.tensor.transpose(vec_t[:, t, :], vec_sorted[:, t, :], ident16[:])
-
-            def sort_x(c):
-                nc.vector.tensor_copy(
-                    out=x_sorted[:, c, :].bitcast(F32).rearrange("a (g t q w) -> a g t q w", g=GROUPS, t=PACK, w=4),
-                    in_=x_raw[:, c, :].bitcast(F32).rearrange("a (g q t w) -> a g t q w", g=GROUPS, t=PACK, w=4),
-                )
-
+            transpose_x_words(0)
+            transpose_x_words(1)
             nc.vector.tensor_scalar(
                 out=w_parts[:, 0, :, :], in0=vec_t[:, :, 0:UNITS], scalar1=LN_LOW, scalar2=LN_HIGH,
                 op0=ALU.max, op1=ALU.min,
             )
-            sort_x(0)
-            nc.vector.reciprocal(out=w_inverse[:], in_=w_parts[:, 0, :, :])
-            sort_x(1)
-            nc.vector.tensor_tensor(out=w_parts[:, 1, :, :], in0=vec_t[:, :, 0:UNITS], in1=w_inverse[:], op=ALU.mult)
             nc.vector.tensor_copy(out=gain[:], in_=vec_t[:, :, 64 : 64 + UNITS])
+            nc.vector.reciprocal(out=w_inverse[:], in_=w_parts[:, 0, :, :])
+            transpose_x_words(2)
+            nc.vector.tensor_tensor(out=w_parts[:, 1, :, :], in0=vec_t[:, :, 0:UNITS], in1=w_inverse[:], op=ALU.mult)
             nc.scalar.activation(out=ln_parts[:], in_=w_parts[:], func=ACT.Ln)
-            sort_x(2)
-            sort_x(3)
+            pack_x(0)
+            transpose_x_words(3)
+            pack_x(1)
+            sort_x(0, nc.vector.tensor_copy)
+            sort_x(1, nc.vector.tensor_copy)
 
-            x_packed_words = x_packed[:].rearrange("p g n t -> p (g n t)").bitcast(F32).rearrange(
-                "p (g n u) -> p g n u", g=GROUPS, u=2
-            )
-            for c in range(TOK_TILES):
-                words = x_raw[:, c, :].bitcast(F32)
-                bank = psum.tile([P, GROUPS, 2, P], F32, name="x_words_t", tag="mm")
-                for g in range(GROUPS):
-                    for u in range(2):
-                        nc.tensor.transpose(bank[:, g, u, :], words[:, 256 * g + u : 256 * (g + 1) : 2], ident32[:])
-                nc.scalar.copy(
-                    out=x_packed_words[:, :, c * P : (c + 1) * P, :], in_=bank[:].rearrange("p g u n -> p g n u")
-                )
-
-            def sort_w(h):
+            def sort_w_codes(h):
                 nc.vector.tensor_copy(
                     out=w_codes[:, h, :, :].rearrange("p a n -> p (a n)").bitcast(I32).rearrange(
                         "p (b t q w) -> p b t q w", t=PACK, q=16, w=4
@@ -152,6 +172,8 @@ def tile_draft_heads_shared_unembedding_k7_kernel(
                         "p (b q t w) -> p b t q w", t=PACK, q=16, w=4
                     ),
                 )
+
+            def sort_w_scale(h):
                 nc.vector.tensor_copy(
                     out=w_scale[:, h, :, :].rearrange("p a n -> p (a n)").bitcast(I32).rearrange(
                         "p (b t q w) -> p b t q w", t=PACK, q=16, w=2
@@ -161,25 +183,34 @@ def tile_draft_heads_shared_unembedding_k7_kernel(
                     ),
                 )
 
-            sort_w(0)
-            for g in range(GROUPS):
+            def sort_w(h):
+                sort_w_codes(h)
+                sort_w_scale(h)
+
+            def quantize_x(g):
                 nc.vector.quantize_mx(
                     out=x_codes[:, g, :].bitcast(FP8X4),
                     scales=x_scale[:, g, :],
                     in_=x_packed[:, g, :, :].rearrange("p n t -> p (n t)"),
                 )
-            nc.vector.tensor_tensor(out=ln_w[:], in0=ln_parts[:, 0, :, :], in1=ln_parts[:, 1, :, :], op=ALU.add)
 
-            for g in range(GROUPS):
-                for half in range(2):
-                    bank = psum.tile([P, 2, TOKENS], BF16, name="x_res_t", tag="tr")
-                    for tt in range(2):
-                        col = g * PASS + (2 * half + tt) * P
-                        for c in range(TOK_TILES):
-                            nc.tensor.transpose(
-                                bank[:, tt, c * P : (c + 1) * P], x_sorted[:, c, col : col + P], ident16[:]
-                            )
-                    nc.scalar.copy(out=x_res[:, g, 2 * half : 2 * half + 2, :], in_=bank[:])
+            def transpose_x_residual(g, half):
+                bank = psum.tile([P, 2, TOKENS], BF16, name="x_res_t", tag="tr")
+                for tt in range(2):
+                    col = g * PASS + (2 * half + tt) * P
+                    for c in range(TOK_TILES):
+                        nc.tensor.transpose(
+                            bank[:, tt, c * P : (c + 1) * P], x_sorted[:, c, col : col + P], ident16[:]
+                        )
+                nc.scalar.copy(out=x_res[:, g, 2 * half : 2 * half + 2, :], in_=bank[:])
+
+            sort_w_codes(0)
+            sort_w_scale(0)
+            quantize_x(0)
+            quantize_x(1)
+            sort_x(2, nc.vector.tensor_copy)
+            sort_x(3, nc.vector.tensor_copy)
+            nc.vector.tensor_tensor(out=ln_w[:], in0=ln_parts[:, 0, :, :], in1=ln_parts[:, 1, :, :], op=ALU.add)
 
             silu = {}
 
@@ -251,135 +282,187 @@ def tile_draft_heads_shared_unembedding_k7_kernel(
                 )
 
             project(0)
-            sort_w(1)
+            transpose_x_residual(0, 0)
+            transpose_x_residual(0, 1)
             project(1)
-            sort_w(2)
+            transpose_x_residual(1, 0)
+            transpose_x_residual(1, 1)
+            pack_u(0, 0)
+            pack_u(0, 1)
+            quantize_u(0, 0)
+            sort_w(1)
+            quantize_u(0, 1)
+            project(2)
+            project(3)
             residual(0)
-            sort_w(3)
+            pack_u(1, 0)
             pack_hidden(0)
-            for u in range(2, 6):
-                project(u)
+            sort_w(2)
+            project(4)
+            project(5)
+            quantize_u(1, 0)
             residual(1)
             quantize_hidden(0)
+            sort_w(3)
+            project(6)
+            project(7)
             pack_hidden(1)
-            for u in range(6, UNITS):
-                project(u)
-            pack_u(0, 0)
-            quantize_hidden(1)
-            pack_u(1, 0)
-            quantize_u(0, 0)
-            pack_u(0, 1)
-            quantize_u(1, 0)
             pack_u(1, 1)
-            quantize_u(0, 1)
+            quantize_hidden(1)
             residual(2)
             quantize_u(1, 1)
         late = ctx.enter_context(tc.tile_pool(name="late", bufs=1))
         y_scale = late.tile([P, GROUPS, HEADS * TOKENS], U8, name="y_scale", align_bytes=64)
 
         y_t, y_packed, y_banks, y_rows, logits = {}, {}, {}, {}, {}
+        last = UNITS - 1
 
-        def unembed_matmuls(u):
+        def unembed_matmuls(i):
+            u, t = divmod(i, PACK)
             h, g = divmod(u, GROUPS)
-            for t in range(PACK):
-                col = g * PASS + t * P
-                logits[u, t] = psum.tile([P, TOKENS], F32, name="logits", tag="mm")
-                for kg in range(GROUPS):
-                    nc.tensor.matmul_mx(
-                        out=logits[u, t][:],
-                        lhsT=u_codes[:, kg, col : col + P].bitcast(FP8X4),
-                        lhsT_scale=u_scale[:, kg, col : col + P],
-                        rhs=h_codes[GROUPS * h + kg][:].bitcast(FP8X4),
-                        rhs_scale=h_scale[GROUPS * h + kg][:],
-                        start=(kg == 0),
-                        stop=(kg == GROUPS - 1),
-                    )
-
-        def soft_cap(u):
-            y_t[u] = keep.tile([P, PACK, TOKENS], F32, name="y_t", tag="y_t", bufs=3)
-            for t in range(PACK):
-                nc.scalar.activation(out=y_t[u][:, t, :], in_=logits[u, t][:], func=ACT.Tanh)
-
-        def weigh(u):
-            for t in range(PACK):
-                nc.scalar.activation(
-                    out=y_t[u][:, t, :], in_=y_t[u][:, t, :], func=ACT.Exp, bias=ln_w[:, t, u : u + 1], scale=CAP
+            col = g * PASS + t * P
+            logits[i] = psum.tile([P, TOKENS], F32, name="logits", tag="mm")
+            for kg in range(GROUPS):
+                nc.tensor.matmul_mx(
+                    out=logits[i][:],
+                    lhsT=u_codes[:, kg, col : col + P].bitcast(FP8X4),
+                    lhsT_scale=u_scale[:, kg, col : col + P],
+                    rhs=h_codes[GROUPS * h + kg][:].bitcast(FP8X4),
+                    rhs_scale=h_scale[GROUPS * h + kg][:],
+                    start=(kg == 0),
+                    stop=(kg == GROUPS - 1),
                 )
 
-        def transpose_y(u):
-            for c in range(TOK_TILES):
-                y_banks[u, c] = psum.tile([P, PACK, P], F32, name="y_bank", tag="tr")
-                for t in range(PACK):
-                    nc.tensor.transpose(y_banks[u, c][:, t, :], y_t[u][:, t, c * P : (c + 1) * P], ident32[:])
+        def soft_cap(i):
+            u, t = divmod(i, PACK)
+            if t == 0:
+                y_t[u] = keep.tile([P, PACK, TOKENS], F32, name="y_t", tag="y_t", bufs=3)
+            nc.scalar.activation(out=y_t[u][:, t, :], in_=logits[i][:], func=ACT.Tanh)
 
-        def store_rows(u):
+        def weigh(i, toks):
+            u, t = divmod(i, PACK)
+            nc.scalar.activation(
+                out=y_t[u][:, t, toks], in_=y_t[u][:, t, toks], func=ACT.Exp, bias=ln_w[:, t, u : u + 1], scale=CAP
+            )
+
+        def transpose_y(u, c):
+            if c == 0:
+                y_rows[u] = late.tile([P, TOK_TILES, PASS], F32, name="y_rows", tag="y_rows", bufs=3)
+            y_banks[u, c] = psum.tile([P, PACK, P], F32, name="y_bank", tag="tr")
+            for t in range(PACK):
+                nc.tensor.transpose(y_banks[u, c][:, t, :], y_t[u][:, t, c * P : (c + 1) * P], ident32[:])
+
+        def store_rows(u, c, copy):
             h, g = divmod(u, GROUPS)
-            copy = nc.scalar.copy if u in SCALAR_EVAC_UNITS else nc.vector.tensor_copy
-            y_rows[u] = late.tile([P, TOK_TILES, PASS], F32, name="y_rows", tag="y_rows", bufs=3)
             dest = out_0[h, :, g * PASS : (g + 1) * PASS].rearrange("(c p) v -> p c v", p=P)
-            for c in range(TOK_TILES):
-                copy(
-                    out=y_rows[u][:, c, :].rearrange("a (p t) -> a p t", t=PACK),
-                    in_=y_banks[u, c][:].rearrange("a t p -> a p t"),
+            copy(
+                out=y_rows[u][:, c, :].rearrange("a (p t) -> a p t", t=PACK),
+                in_=y_banks[u, c][:].rearrange("a t p -> a p t"),
+            )
+            nc.sync.dma_start(out=dest[:, c, :], in_=y_rows[u][:, c, :])
+
+        def pack_y(u, toks):
+            if toks.start == 0:
+                y_packed[u] = late.tile(
+                    [P, TOKENS, PACK], BF16, name="y_packed", tag="y_packed", bufs=2, align_bytes=64
                 )
-                if u == UNITS - 1:
-                    nc.sync.dma_start(out=dest[:, c, :], in_=y_rows[u][:, c, :])
-            if u < UNITS - 1:
-                nc.sync.dma_start(out=dest, in_=y_rows[u][:])
+            interleave(y_packed[u][:, toks, :], y_t[u][:, :, toks])
 
-        def pack_y(u):
-            y_packed[u] = late.tile([P, TOKENS, PACK], BF16, name="y_packed", tag="y_packed", bufs=2, align_bytes=64)
-            interleave(y_packed[u][:], y_t[u][:])
-
-        def quantize_y(u):
+        def quantize_y(u, toks):
             h, g = divmod(u, GROUPS)
-            y_codes = late.tile([P, TOKENS], U32, name="y_codes", tag="y_codes", bufs=3, align_bytes=64)
+            cols = slice(h * TOKENS + toks.start, h * TOKENS + toks.stop)
+            y_codes = late.tile(
+                [P, toks.stop - toks.start], U32, name="y_codes", tag="y_codes", bufs=3, align_bytes=64
+            )
             nc.vector.quantize_mx(
                 out=y_codes[:].bitcast(FP8X4),
-                scales=y_scale[:, g, h * TOKENS : (h + 1) * TOKENS],
-                in_=y_packed[u][:].rearrange("p n t -> p (n t)"),
+                scales=y_scale[:, g, cols],
+                in_=y_packed[u][:, toks, :].rearrange("p n t -> p (n t)"),
             )
             nc.sync.dma_start(
-                out=out_1[g].rearrange("p m t -> p (m t)")[:, PACK * h * TOKENS : PACK * (h + 1) * TOKENS].bitcast(I32),
+                out=out_1[g].rearrange("p m t -> p (m t)")[:, PACK * cols.start : PACK * cols.stop].bitcast(I32),
                 in_=y_codes[:].bitcast(I32),
             )
 
-        def store_scales(first, last):
-            cols = slice(first * TOKENS, last * TOKENS)
+        def store_scales(first, stop):
+            cols = slice(first * TOKENS, stop * TOKENS)
             for q in range(4):
                 nc.sync.dma_start(
                     out=out_2[:, 4 * q : 4 * q + 4, cols].rearrange("g r m -> r g m").bitcast(I32),
                     in_=y_scale[32 * q : 32 * q + 4, :, cols].bitcast(I32),
                 )
 
-        unembed_matmuls(0)
+        every = slice(0, TOKENS)
+
+        def vector_block(u):
+            if u < last - 1:
+                pack_y(u, every)
+            if u + 4 < UNITS:
+                quantize_hidden(u + 4)
+            if u + 5 < UNITS:
+                residual(u + 5)
+            for c in range(TOK_TILES):
+                if TOK_TILES * u + c >= SCALAR_EVACS:
+                    store_rows(u, c, nc.vector.tensor_copy)
+            if u == last - 1:
+                pack_y(u, every)
+            else:
+                quantize_y(u, every)
+            if u + 5 < UNITS:
+                pack_hidden(u + 5)
+            if u == 3:
+                store_scales(0, 2)
+            if u == 5:
+                store_scales(2, 3)
+
+        for i in range(PACK):
+            unembed_matmuls(i)
         soft_cap(0)
-        unembed_matmuls(1)
-        weigh(0)
+        unembed_matmuls(PACK)
         pack_hidden(2)
         residual(3)
         quantize_hidden(2)
         pack_hidden(3)
-        for u in range(UNITS):
-            transpose_y(u)
-            pack_y(u)
-            if u + 3 < UNITS:
-                quantize_hidden(u + 3)
-            if u + 1 < UNITS:
-                soft_cap(u + 1)
-            if u + 2 < UNITS:
-                unembed_matmuls(u + 2)
-            if u == UNITS - 1:
-                quantize_y(u)
-                store_scales(HEADS - 1, HEADS)
-            store_rows(u)
-            if u + 1 < UNITS:
-                weigh(u + 1)
-            if u + 4 < UNITS:
-                residual(u + 4)
-            if u < UNITS - 1:
-                quantize_y(u)
-            if u + 4 < UNITS:
-                pack_hidden(u + 4)
-            if u == UNITS - 3:
-                store_scales(0, HEADS - 1)
+        residual(4)
+        quantize_hidden(3)
+        pack_hidden(4)
+        for i in range(STEPS - PACK):
+            u, t = divmod(i, PACK)
+            soft_cap(i + 1)
+            if i + 5 < STEPS and i not in (3, 4):
+                unembed_matmuls(i + 5)
+            weigh(i, every)
+            if t == PACK - 1:
+                transpose_y(u, 0)
+                transpose_y(u, 1)
+            if t == 0 and u > 0:
+                transpose_y(u - 1, 2)
+                transpose_y(u - 1, 3)
+                if i == 4:
+                    unembed_matmuls(8)
+                    unembed_matmuls(9)
+                vector_block(u - 1)
+            if 0 <= i - PACK < SCALAR_EVACS:
+                store_rows(u - 1, t, nc.scalar.copy)
+
+        first_half, second_half = slice(0, HALF), slice(HALF, TOKENS)
+        soft_cap(STEPS - 3)
+        transpose_y(last - 1, 2)
+        transpose_y(last - 1, 3)
+        vector_block(last - 1)
+        soft_cap(STEPS - 2)
+        soft_cap(STEPS - 1)
+        for c in range(TOK_TILES):
+            for t in range(PACK):
+                weigh(STEPS - PACK + t, slice(c * P, (c + 1) * P))
+            transpose_y(last, c)
+            if c > 0:
+                store_rows(last, c - 1, nc.scalar.copy)
+            if c == 2:
+                pack_y(last, first_half)
+                quantize_y(last - 1, every)
+        quantize_y(last, first_half)
+        pack_y(last, second_half)
+        store_rows(last, TOK_TILES - 1, nc.scalar.copy)
+        quantize_y(last, second_half)
+        store_scales(HEADS - 1, HEADS)

@@ -24,7 +24,7 @@ GROUPS = D // PASS
 TOK_TILES = TOKENS // P
 UNITS = HEADS * GROUPS
 LN_LOW, LN_HIGH = 2.0**-63, 2.0**63
-SCALAR_EVACS = 11
+SCALAR_EVACS = 7
 STEPS = UNITS * PACK
 HALF = TOKENS // 2
 
@@ -314,7 +314,7 @@ def tile_draft_heads_shared_unembedding_k7_kernel(
         late = ctx.enter_context(tc.tile_pool(name="late", bufs=1))
         y_scale = late.tile([P, GROUPS, HEADS * TOKENS], U8, name="y_scale", align_bytes=64)
 
-        y_t, y_packed, y_banks, y_rows, logits = {}, {}, {}, {}, {}
+        y_t, y_packed, y_banks, y_rows, y_codes, logits = {}, {}, {}, {}, {}, {}
         last = UNITS - 1
 
         def unembed_matmuls(i):
@@ -371,17 +371,21 @@ def tile_draft_heads_shared_unembedding_k7_kernel(
         def quantize_y(u, toks):
             h, g = divmod(u, GROUPS)
             cols = slice(h * TOKENS + toks.start, h * TOKENS + toks.stop)
-            y_codes = late.tile(
-                [P, toks.stop - toks.start], U32, name="y_codes", tag="y_codes", bufs=3, align_bytes=64
+            y_codes[u, toks.start] = late.tile(
+                [P, toks.stop - toks.start], U32, name="y_codes", tag="y_codes", bufs=4, align_bytes=64
             )
             nc.vector.quantize_mx(
-                out=y_codes[:].bitcast(FP8X4),
+                out=y_codes[u, toks.start][:].bitcast(FP8X4),
                 scales=y_scale[:, g, cols],
                 in_=y_packed[u][:, toks, :].rearrange("p n t -> p (n t)"),
             )
+
+        def store_codes(u, toks):
+            h, g = divmod(u, GROUPS)
+            cols = slice(h * TOKENS + toks.start, h * TOKENS + toks.stop)
             nc.sync.dma_start(
                 out=out_1[g].rearrange("p m t -> p (m t)")[:, PACK * cols.start : PACK * cols.stop].bitcast(I32),
-                in_=y_codes[:].bitcast(I32),
+                in_=y_codes[u, toks.start][:].bitcast(I32),
             )
 
         def store_scales(first, stop):
@@ -410,10 +414,6 @@ def tile_draft_heads_shared_unembedding_k7_kernel(
                 quantize_y(u, every)
             if u + 5 < UNITS:
                 pack_hidden(u + 5)
-            if u == 3:
-                store_scales(0, 2)
-            if u == 5:
-                store_scales(2, 3)
 
         for i in range(PACK):
             unembed_matmuls(i)
@@ -444,6 +444,12 @@ def tile_draft_heads_shared_unembedding_k7_kernel(
                 vector_block(u - 1)
             if 0 <= i - PACK < SCALAR_EVACS:
                 store_rows(u - 1, t, nc.scalar.copy)
+            if t == PACK - 1 and u > 0:
+                store_codes(u - 1, every)
+                if u - 1 == 3:
+                    store_scales(0, 2)
+                if u - 1 == 5:
+                    store_scales(2, 3)
 
         first_half, second_half = slice(0, HALF), slice(HALF, TOKENS)
         soft_cap(STEPS - 3)
@@ -461,8 +467,11 @@ def tile_draft_heads_shared_unembedding_k7_kernel(
             if c == 2:
                 pack_y(last, first_half)
                 quantize_y(last - 1, every)
+                store_codes(last - 1, every)
         quantize_y(last, first_half)
+        store_codes(last, first_half)
         pack_y(last, second_half)
         store_rows(last, TOK_TILES - 1, nc.scalar.copy)
         quantize_y(last, second_half)
+        store_codes(last, second_half)
         store_scales(HEADS - 1, HEADS)

@@ -21,12 +21,17 @@ P = 128
 PACK = 4
 PASS = P * PACK
 GROUPS = D // PASS
+RUN = 8
+BLOCKS = P // RUN
+QUADRANTS, SCALE_ROWS = 4, 4
 TOK_TILES = TOKENS // P
 UNITS = HEADS * GROUPS
-LN_LOW, LN_HIGH = 2.0**-63, 2.0**63
-SCALAR_EVACS = 7
 STEPS = UNITS * PACK
-HALF = TOKENS // 2
+BANKS = 4
+GAIN_ROW = 64
+LN_LOW, LN_HIGH = 2.0**-63, 2.0**64
+SCALAR_BANKS = 10
+HIDDEN_LEAD = 5
 
 
 def tile_draft_heads_shared_unembedding_k7_kernel(
@@ -35,10 +40,10 @@ def tile_draft_heads_shared_unembedding_k7_kernel(
     nc = tc.nc
     with ExitStack() as ctx:
         keep = ctx.enter_context(tc.tile_pool(name="keep", bufs=1))
-        psum = ctx.enter_context(tc.psum_pool(name="psum", bufs=4))
+        psum = ctx.enter_context(tc.psum_pool(name="psum", bufs=BANKS))
         ctx.enter_context(tc.manual_schedule())
-        with tc.tile_pool(name="early", bufs=1) as early:
 
+        with tc.tile_pool(name="early", bufs=1) as early:
             ident32 = keep.tile([P, P], F32, name="ident32")
             ident16 = keep.tile([P, P], BF16, name="ident16")
             gain = keep.tile([P, PACK, UNITS], F32, name="gain")
@@ -57,15 +62,20 @@ def tile_draft_heads_shared_unembedding_k7_kernel(
             w_inverse = early.tile([P, PACK, UNITS], F32, name="w_inverse")
             ln_parts = early.tile([P, 2, PACK, UNITS], F32, name="ln_parts")
             x_raw = early.tile([P, TOK_TILES, D], BF16, name="x_raw")
-            x_words = early.tile([P, TOK_TILES, GROUPS, 2, P], F32, name="x_words")
+            x_words = early.tile([P, GROUPS, TOK_TILES, 2, P], F32, name="x_words")
             x_sorted = early.tile([P, TOK_TILES, D], BF16, name="x_sorted")
             x_packed = early.tile([P, GROUPS, TOKENS, PACK], BF16, name="x_packed", align_bytes=64)
             w_codes_raw = early.tile([P, HEADS, GROUPS, 2 * D], U8, name="w_codes_raw")
             w_scale_raw = early.tile([P, HEADS * GROUPS, D], U8, name="w_scale_raw")
             u_raw = early.tile([P, GROUPS, PACK, VOCAB], BF16, name="u_raw")
 
-            def load_x(c):
-                nc.sync.dma_start(out=x_raw[:, c, :], in_=x[c * P : (c + 1) * P, :])
+
+            def load_x(g, pair):
+                toks = slice(2 * pair * P, 2 * (pair + 1) * P)
+                feats = slice(g * PASS, (g + 1) * PASS)
+                nc.sync.dma_start(
+                    out=x_raw[:, 2 * pair : 2 * pair + 2, feats], in_=x[toks, feats].rearrange("(c p) d -> p c d", p=P)
+                )
 
             def load_w(h):
                 nc.sync.dma_start(
@@ -73,119 +83,66 @@ def tile_draft_heads_shared_unembedding_k7_kernel(
                     in_=w_words[GROUPS * h : GROUPS * (h + 1), :, :].rearrange("a p n -> p a n").bitcast(I32),
                 )
 
-            def load_w_scale(first, last):
-                rows = slice(GROUPS * first, GROUPS * last)
-                nc.vector.memset(w_scale_raw[:, rows, :].rearrange("p a n -> p (a n)").bitcast(I32), 0)
-                for q in range(4):
+            def load_w_scale(first, stop):
+                passes = slice(GROUPS * first, GROUPS * stop)
+                nc.vector.memset(w_scale_raw[:, passes, :].rearrange("p a n -> p (a n)").bitcast(I32), 0)
+                for quad in range(QUADRANTS):
+                    rows = slice(SCALE_ROWS * quad, SCALE_ROWS * (quad + 1))
                     nc.sync.dma_start(
-                        out=w_scale_raw[32 * q : 32 * q + 4, rows, :].bitcast(I32),
-                        in_=w_scales[rows, 4 * q : 4 * q + 4, :].rearrange("a r n -> r a n").bitcast(I32),
+                        out=w_scale_raw[32 * quad : 32 * quad + SCALE_ROWS, passes, :].bitcast(I32),
+                        in_=w_scales[passes, rows, :].rearrange("a r n -> r a n").bitcast(I32),
                     )
 
             def load_u(kg):
-                rows = unembed[kg * PASS : (kg + 1) * PASS, :].rearrange("(q t r) v -> t q r v", t=PACK, r=8)
+                rows = unembed[kg * PASS : (kg + 1) * PASS, :].rearrange("(q t r) v -> t q r v", t=PACK, r=RUN)
                 for t in range(PACK):
                     nc.sync.dma_start(out=u_raw[:, kg, t, :], in_=rows[t])
 
             nc.gpsimd.memset(vec[:].bitcast(I32), 0)
-            nc.sync.dma_start(out=vec[0:UNITS, :], in_=token_weight.rearrange("h (g v) -> (h g) v", g=GROUPS))
-            nc.sync.dma_start(out=vec[64 : 64 + UNITS, :], in_=branch_gain.rearrange("h (g v) -> (h g) v", g=GROUPS))
-            load_x(0)
-            load_x(1)
-            load_x(2)
-            load_x(3)
             make_identity(nc, ident16[:])
             make_identity(nc, ident32[:])
+            nc.sync.dma_start(out=vec[0:UNITS, :], in_=token_weight.rearrange("h (g v) -> (h g) v", g=GROUPS))
+            nc.sync.dma_start(
+                out=vec[GAIN_ROW : GAIN_ROW + UNITS, :], in_=branch_gain.rearrange("h (g v) -> (h g) v", g=GROUPS)
+            )
+            for g in range(GROUPS):
+                for pair in range(TOK_TILES // 2):
+                    load_x(g, pair)
             load_w(0)
             load_w_scale(0, 1)
             load_u(0)
-            load_w_scale(1, HEADS)
             load_w(1)
+            load_w_scale(1, 2)
             load_u(1)
             load_w(2)
+            load_w_scale(2, HEADS)
             load_w(3)
 
-            x_packed_words = x_packed[:].rearrange("p g n t -> p (g n t)").bitcast(F32).rearrange(
-                "p (g n u) -> p g n u", g=GROUPS, u=2
+
+            x_packed_pairs = (
+                x_packed[:].rearrange("p g n t -> p (g n t)").bitcast(F32).rearrange("p (g n half) -> p g n half", g=GROUPS, half=2)
             )
-            word_banks = {}
+            pair_banks = {}
 
-            def sort_x(c, copy):
-                copy(
-                    out=x_sorted[:, c, :].bitcast(F32).rearrange("a (g t q w) -> a g t q w", t=PACK, q=16, w=4),
-                    in_=x_raw[:, c, :].bitcast(F32).rearrange("a (g q t w) -> a g t q w", t=PACK, q=16, w=4),
-                )
-
-            def transpose_x_words(c):
+            def transpose_x_pairs(g, pair):
+                tiles = slice(2 * pair, 2 * pair + 2)
                 nc.vector.tensor_copy(
-                    out=x_words[:, c, :, :, :],
-                    in_=x_raw[:, c, :].bitcast(F32).rearrange("a (g p u) -> a g u p", g=GROUPS, u=2),
+                    out=x_words[:, g, tiles, :, :],
+                    in_=x_raw[:, tiles, g * PASS : (g + 1) * PASS].bitcast(F32).rearrange("a c (p half) -> a c half p", half=2),
                 )
-                for g in range(GROUPS):
-                    if c % 2 == 0:
-                        word_banks[c // 2, g] = psum.tile([P, 2, 2, P], F32, name="x_words_t", tag="mm")
-                    for u in range(2):
-                        nc.tensor.transpose(word_banks[c // 2, g][:, c % 2, u, :], x_words[:, c, g, u, :], ident32[:])
+                pair_banks[g, pair] = psum.tile([P, 2, 2, P], F32, name="x_words_t", tag="mm")
+                for c in range(2):
+                    for half in range(2):
+                        nc.tensor.transpose(
+                            pair_banks[g, pair][:, c, half, :], x_words[:, g, 2 * pair + c, half, :], ident32[:]
+                        )
 
-            def pack_x(pair):
-                for g in range(GROUPS):
-                    nc.scalar.copy(
-                        out=x_packed_words[:, g, 2 * pair * P : 2 * (pair + 1) * P, :].rearrange(
-                            "p (c n) u -> p c n u", c=2
-                        ),
-                        in_=word_banks[pair, g][:].rearrange("p c u n -> p c n u"),
-                    )
-
-            nc.vector.tensor_copy(
-                out=vec_sorted[0:64, :, :], in_=vec[0:64, :].rearrange("a (p t) -> a t p", t=PACK)
-            )
-            nc.vector.tensor_copy(
-                out=vec_sorted[64:128, :, :].rearrange("a t (q r) -> a t q r", r=8),
-                in_=vec[64:128, :].rearrange("a (q t r) -> a t q r", t=PACK, r=8),
-            )
-            vec_t = psum.tile([P, PACK, P], BF16, name="vec_t", tag="tr")
-            for t in range(PACK):
-                nc.tensor.transpose(vec_t[:, t, :], vec_sorted[:, t, :], ident16[:])
-            transpose_x_words(0)
-            transpose_x_words(1)
-            nc.vector.tensor_scalar(
-                out=w_parts[:, 0, :, :], in0=vec_t[:, :, 0:UNITS], scalar1=LN_LOW, scalar2=LN_HIGH,
-                op0=ALU.max, op1=ALU.min,
-            )
-            nc.vector.tensor_copy(out=gain[:], in_=vec_t[:, :, 64 : 64 + UNITS])
-            nc.vector.reciprocal(out=w_inverse[:], in_=w_parts[:, 0, :, :])
-            transpose_x_words(2)
-            nc.vector.tensor_tensor(out=w_parts[:, 1, :, :], in0=vec_t[:, :, 0:UNITS], in1=w_inverse[:], op=ALU.mult)
-            nc.scalar.activation(out=ln_parts[:], in_=w_parts[:], func=ACT.Ln)
-            pack_x(0)
-            transpose_x_words(3)
-            pack_x(1)
-            sort_x(0, nc.vector.tensor_copy)
-            sort_x(1, nc.vector.tensor_copy)
-
-            def sort_w_codes(h):
-                nc.vector.tensor_copy(
-                    out=w_codes[:, h, :, :].rearrange("p a n -> p (a n)").bitcast(I32).rearrange(
-                        "p (b t q w) -> p b t q w", t=PACK, q=16, w=4
-                    ),
-                    in_=w_codes_raw[:, h, :, :].rearrange("p a n -> p (a n)").bitcast(I32).rearrange(
-                        "p (b q t w) -> p b t q w", t=PACK, q=16, w=4
-                    ),
+            def pack_x(g, pair):
+                toks = slice(2 * pair * P, 2 * (pair + 1) * P)
+                nc.scalar.copy(
+                    out=x_packed_pairs[:, g, toks, :].rearrange("p (c n) half -> p c n half", c=2),
+                    in_=pair_banks[g, pair][:].rearrange("p c half n -> p c n half"),
                 )
-
-            def sort_w_scale(h):
-                nc.vector.tensor_copy(
-                    out=w_scale[:, h, :, :].rearrange("p a n -> p (a n)").bitcast(I32).rearrange(
-                        "p (b t q w) -> p b t q w", t=PACK, q=16, w=2
-                    ),
-                    in_=w_scale_raw[:, GROUPS * h : GROUPS * (h + 1), :].rearrange("p a n -> p (a n)").bitcast(I32).rearrange(
-                        "p (b q t w) -> p b t q w", t=PACK, q=16, w=2
-                    ),
-                )
-
-            def sort_w(h):
-                sort_w_codes(h)
-                sort_w_scale(h)
 
             def quantize_x(g):
                 nc.vector.quantize_mx(
@@ -194,29 +151,55 @@ def tile_draft_heads_shared_unembedding_k7_kernel(
                     in_=x_packed[:, g, :, :].rearrange("p n t -> p (n t)"),
                 )
 
-            def transpose_x_residual(g, half):
-                bank = psum.tile([P, 2, TOKENS], BF16, name="x_res_t", tag="tr")
-                for tt in range(2):
-                    col = g * PASS + (2 * half + tt) * P
-                    for c in range(TOK_TILES):
-                        nc.tensor.transpose(
-                            bank[:, tt, c * P : (c + 1) * P], x_sorted[:, c, col : col + P], ident16[:]
-                        )
-                nc.scalar.copy(out=x_res[:, g, 2 * half : 2 * half + 2, :], in_=bank[:])
 
-            sort_w_codes(0)
-            sort_w_scale(0)
-            quantize_x(0)
-            quantize_x(1)
-            sort_x(2, nc.vector.tensor_copy)
-            sort_x(3, nc.vector.tensor_copy)
-            nc.vector.tensor_tensor(out=ln_w[:], in0=ln_parts[:, 0, :, :], in1=ln_parts[:, 1, :, :], op=ALU.add)
+            def sort_runs(dst, src, run_words):
+                nc.vector.tensor_copy(
+                    out=dst.rearrange("p (b t q w) -> p b t q w", t=PACK, q=BLOCKS, w=run_words),
+                    in_=src.rearrange("p (b q t w) -> p b t q w", t=PACK, q=BLOCKS, w=run_words),
+                )
 
-            silu = {}
+            def sort_w_codes(h):
+                sort_runs(
+                    w_codes[:, h, :, :].rearrange("p a n -> p (a n)").bitcast(I32),
+                    w_codes_raw[:, h, :, :].rearrange("p a n -> p (a n)").bitcast(I32),
+                    RUN * 2 // 4,
+                )
+
+            def sort_w_scale(h):
+                sort_runs(
+                    w_scale[:, h, :, :].rearrange("p a n -> p (a n)").bitcast(I32),
+                    w_scale_raw[:, GROUPS * h : GROUPS * (h + 1), :].rearrange("p a n -> p (a n)").bitcast(I32),
+                    RUN // 4,
+                )
+
+            def sort_w(h):
+                sort_w_codes(h)
+                sort_w_scale(h)
+
+            def sort_x(g):
+                feats = slice(g * PASS, (g + 1) * PASS)
+                nc.vector.tensor_copy(
+                    out=x_sorted[:, :, feats].bitcast(F32).rearrange("a c (t q w) -> a c t q w", t=PACK, q=BLOCKS),
+                    in_=x_raw[:, :, feats].bitcast(F32).rearrange("a c (q t w) -> a c t q w", t=PACK, q=BLOCKS),
+                )
+
+            def transpose_x_residual(g):
+                for first in range(0, PACK, 2):
+                    bank = psum.tile([P, 2, TOKENS], BF16, name="x_res_t", tag="tr")
+                    for t in range(first, first + 2):
+                        col = g * PASS + t * P
+                        for c in range(TOK_TILES):
+                            nc.tensor.transpose(
+                                bank[:, t - first, c * P : (c + 1) * P], x_sorted[:, c, col : col + P], ident16[:]
+                            )
+                    nc.scalar.copy(out=x_res[:, g, first : first + 2, :], in_=bank[:])
+
+
+            silu, hidden, hidden_packed, h_codes, h_scale = {}, {}, {}, {}, {}
 
             def project(u):
                 h, g = divmod(u, GROUPS)
-                silu[u] = keep.tile([P, PACK, TOKENS], F32, name="silu", tag="silu", bufs=6)
+                silu[u] = keep.tile([P, PACK, TOKENS], F32, name="silu", tag="silu", bufs=UNITS - 2)
                 for t in range(PACK):
                     col = g * PASS + t * P
                     bank = psum.tile([P, TOKENS], F32, name="z", tag="mm")
@@ -232,15 +215,16 @@ def tile_draft_heads_shared_unembedding_k7_kernel(
                         )
                     nc.scalar.activation(out=silu[u][:, t, :], in_=bank[:], func=ACT.Silu)
 
-            hidden, hidden_packed, h_codes, h_scale = {}, {}, {}, {}
-
             def residual(u):
-                g = u % GROUPS
                 hidden[u] = keep.tile([P, PACK, TOKENS], BF16, name="hidden", tag="hidden", bufs=2)
                 for t in range(PACK):
                     nc.vector.scalar_tensor_tensor(
-                        out=hidden[u][:, t, :], in0=silu[u][:, t, :], scalar=gain[:, t, u : u + 1],
-                        in1=x_res[:, g, t, :], op0=ALU.mult, op1=ALU.add,
+                        out=hidden[u][:, t, :],
+                        in0=silu[u][:, t, :],
+                        scalar=gain[:, t, u : u + 1],
+                        in1=x_res[:, u % GROUPS, t, :],
+                        op0=ALU.mult,
+                        op1=ALU.add,
                     )
 
             def interleave(dst, src):
@@ -281,12 +265,43 @@ def tile_draft_heads_shared_unembedding_k7_kernel(
                     in_=u_packed[kg, g][:].rearrange("p t m j -> p (t m j)"),
                 )
 
-            project(0)
-            transpose_x_residual(0, 0)
-            transpose_x_residual(0, 1)
-            project(1)
-            transpose_x_residual(1, 0)
-            transpose_x_residual(1, 1)
+            nc.vector.tensor_copy(
+                out=vec_sorted[0:GAIN_ROW, :, :], in_=vec[0:GAIN_ROW, :].rearrange("a (p t) -> a t p", t=PACK)
+            )
+            nc.vector.tensor_copy(
+                out=vec_sorted[GAIN_ROW:P, :, :].rearrange("a t (q r) -> a t q r", r=RUN),
+                in_=vec[GAIN_ROW:P, :].rearrange("a (q t r) -> a t q r", t=PACK, r=RUN),
+            )
+            vec_t = psum.tile([P, PACK, P], BF16, name="vec_t", tag="tr")
+            for t in range(PACK):
+                nc.tensor.transpose(vec_t[:, t, :], vec_sorted[:, t, :], ident16[:])
+            weight = vec_t[:, :, 0:UNITS]
+
+            transpose_x_pairs(0, 0)
+            nc.vector.tensor_scalar(
+                out=w_parts[:, 0, :, :], in0=weight, scalar1=LN_LOW, scalar2=LN_HIGH, op0=ALU.max, op1=ALU.min
+            )
+            transpose_x_pairs(0, 1)
+            nc.vector.reciprocal(out=w_inverse[:], in_=w_parts[:, 0, :, :])
+            transpose_x_pairs(1, 0)
+            nc.vector.tensor_tensor(out=w_parts[:, 1, :, :], in0=weight, in1=w_inverse[:], op=ALU.mult)
+            nc.scalar.activation(out=ln_parts[:], in_=w_parts[:], func=ACT.Ln)
+            transpose_x_pairs(1, 1)
+            sort_x(0)
+            for g in range(GROUPS):
+                for pair in range(TOK_TILES // 2):
+                    pack_x(g, pair)
+            sort_w_codes(0)
+            quantize_x(0)
+            nc.vector.tensor_copy(out=gain[:], in_=vec_t[:, :, GAIN_ROW : GAIN_ROW + UNITS])
+            sort_w_scale(0)
+            quantize_x(1)
+            sort_x(1)
+            for g in range(GROUPS):
+                project(g)
+                transpose_x_residual(g)
+            nc.vector.tensor_tensor(out=ln_w[:], in0=ln_parts[:, 0, :, :], in1=ln_parts[:, 1, :, :], op=ALU.add)
+
             pack_u(0, 0)
             pack_u(0, 1)
             quantize_u(0, 0)
@@ -311,11 +326,13 @@ def tile_draft_heads_shared_unembedding_k7_kernel(
             quantize_hidden(1)
             residual(2)
             quantize_u(1, 1)
+
+
         late = ctx.enter_context(tc.tile_pool(name="late", bufs=1))
         y_scale = late.tile([P, GROUPS, HEADS * TOKENS], U8, name="y_scale", align_bytes=64)
-
         y_t, y_packed, y_banks, y_rows, y_codes, logits = {}, {}, {}, {}, {}, {}
         last = UNITS - 1
+        every, first_half, second_half = slice(0, TOKENS), slice(0, TOKENS // 2), slice(TOKENS // 2, TOKENS)
 
         def unembed_matmuls(i):
             u, t = divmod(i, PACK)
@@ -354,11 +371,11 @@ def tile_draft_heads_shared_unembedding_k7_kernel(
 
         def store_rows(u, c, copy):
             h, g = divmod(u, GROUPS)
-            dest = out_0[h, :, g * PASS : (g + 1) * PASS].rearrange("(c p) v -> p c v", p=P)
             copy(
                 out=y_rows[u][:, c, :].rearrange("a (p t) -> a p t", t=PACK),
                 in_=y_banks[u, c][:].rearrange("a t p -> a p t"),
             )
+            dest = out_0[h, :, g * PASS : (g + 1) * PASS].rearrange("(c p) v -> p c v", p=P)
             nc.sync.dma_start(out=dest[:, c, :], in_=y_rows[u][:, c, :])
 
         def pack_y(u, toks):
@@ -370,67 +387,69 @@ def tile_draft_heads_shared_unembedding_k7_kernel(
 
         def quantize_y(u, toks):
             h, g = divmod(u, GROUPS)
-            cols = slice(h * TOKENS + toks.start, h * TOKENS + toks.stop)
             y_codes[u, toks.start] = late.tile(
                 [P, toks.stop - toks.start], U32, name="y_codes", tag="y_codes", bufs=4, align_bytes=64
             )
             nc.vector.quantize_mx(
                 out=y_codes[u, toks.start][:].bitcast(FP8X4),
-                scales=y_scale[:, g, cols],
+                scales=y_scale[:, g, h * TOKENS + toks.start : h * TOKENS + toks.stop],
                 in_=y_packed[u][:, toks, :].rearrange("p n t -> p (n t)"),
             )
 
         def store_codes(u, toks):
             h, g = divmod(u, GROUPS)
-            cols = slice(h * TOKENS + toks.start, h * TOKENS + toks.stop)
+            code_bytes = slice(PACK * (h * TOKENS + toks.start), PACK * (h * TOKENS + toks.stop))
             nc.sync.dma_start(
-                out=out_1[g].rearrange("p m t -> p (m t)")[:, PACK * cols.start : PACK * cols.stop].bitcast(I32),
+                out=out_1[g].rearrange("p m t -> p (m t)")[:, code_bytes].bitcast(I32),
                 in_=y_codes[u, toks.start][:].bitcast(I32),
             )
 
         def store_scales(first, stop):
             cols = slice(first * TOKENS, stop * TOKENS)
-            for q in range(4):
+            for quad in range(QUADRANTS):
+                rows = slice(SCALE_ROWS * quad, SCALE_ROWS * (quad + 1))
                 nc.sync.dma_start(
-                    out=out_2[:, 4 * q : 4 * q + 4, cols].rearrange("g r m -> r g m").bitcast(I32),
-                    in_=y_scale[32 * q : 32 * q + 4, :, cols].bitcast(I32),
+                    out=out_2[:, rows, cols].rearrange("g r m -> r g m").bitcast(I32),
+                    in_=y_scale[32 * quad : 32 * quad + SCALE_ROWS, :, cols].bitcast(I32),
                 )
 
-        every = slice(0, TOKENS)
-
-        def vector_block(u):
+        def vector_round(u):
+            ahead = u + HIDDEN_LEAD
             if u < last - 1:
                 pack_y(u, every)
-            if u + 4 < UNITS:
-                quantize_hidden(u + 4)
-            if u + 5 < UNITS:
-                residual(u + 5)
+            if ahead - 1 < UNITS:
+                quantize_hidden(ahead - 1)
+            if ahead < UNITS:
+                residual(ahead)
             for c in range(TOK_TILES):
-                if TOK_TILES * u + c >= SCALAR_EVACS:
+                if TOK_TILES * u + c >= SCALAR_BANKS:
                     store_rows(u, c, nc.vector.tensor_copy)
             if u == last - 1:
                 pack_y(u, every)
             else:
                 quantize_y(u, every)
-            if u + 5 < UNITS:
-                pack_hidden(u + 5)
+            if ahead < UNITS:
+                pack_hidden(ahead)
 
-        for i in range(PACK):
+        for i in range(BANKS):
             unembed_matmuls(i)
         soft_cap(0)
-        unembed_matmuls(PACK)
-        pack_hidden(2)
-        residual(3)
-        quantize_hidden(2)
-        pack_hidden(3)
-        residual(4)
-        quantize_hidden(3)
-        pack_hidden(4)
+        unembed_matmuls(BANKS)
+        for u in range(2, HIDDEN_LEAD - 1):
+            pack_hidden(u)
+            residual(u + 1)
+            quantize_hidden(u)
+        pack_hidden(HIDDEN_LEAD - 1)
+
+        head1 = GROUPS * PACK
+        deferred = (head1, head1 + 1)
+        scale_batches = {3: (0, 2), 5: (2, 3)}
         for i in range(STEPS - PACK):
             u, t = divmod(i, PACK)
             soft_cap(i + 1)
-            if i + 5 < STEPS and i not in (3, 4):
-                unembed_matmuls(i + 5)
+            refill = i + 1 + BANKS
+            if refill < STEPS and refill not in deferred:
+                unembed_matmuls(refill)
             weigh(i, every)
             if t == PACK - 1:
                 transpose_y(u, 0)
@@ -438,24 +457,21 @@ def tile_draft_heads_shared_unembedding_k7_kernel(
             if t == 0 and u > 0:
                 transpose_y(u - 1, 2)
                 transpose_y(u - 1, 3)
-                if i == 4:
-                    unembed_matmuls(8)
-                    unembed_matmuls(9)
-                vector_block(u - 1)
-            if 0 <= i - PACK < SCALAR_EVACS:
+                if u == 1:
+                    for step in deferred:
+                        unembed_matmuls(step)
+                vector_round(u - 1)
+            if 0 <= i - PACK < SCALAR_BANKS:
                 store_rows(u - 1, t, nc.scalar.copy)
             if t == PACK - 1 and u > 0:
                 store_codes(u - 1, every)
-                if u - 1 == 3:
-                    store_scales(0, 2)
-                if u - 1 == 5:
-                    store_scales(2, 3)
+                if u - 1 in scale_batches:
+                    store_scales(*scale_batches[u - 1])
 
-        first_half, second_half = slice(0, HALF), slice(HALF, TOKENS)
         soft_cap(STEPS - 3)
         transpose_y(last - 1, 2)
         transpose_y(last - 1, 3)
-        vector_block(last - 1)
+        vector_round(last - 1)
         soft_cap(STEPS - 2)
         soft_cap(STEPS - 1)
         for c in range(TOK_TILES):
@@ -464,7 +480,7 @@ def tile_draft_heads_shared_unembedding_k7_kernel(
             transpose_y(last, c)
             if c > 0:
                 store_rows(last, c - 1, nc.scalar.copy)
-            if c == 2:
+            if c == TOK_TILES - 2:
                 pack_y(last, first_half)
                 quantize_y(last - 1, every)
                 store_codes(last - 1, every)

from contextlib import ExitStack

import concourse.mybir as mybir
from concourse.masks import make_identity

HEADS, TOKENS, D, VOCAB = 4, 512, 1024, 1024
CAP = 2.0
FLOPS = 2 * HEADS * TOKENS * D * (D + VOCAB)

F32 = mybir.dt.float32
BF16 = mybir.dt.bfloat16
I32 = mybir.dt.int32
U32 = mybir.dt.uint32
U8 = mybir.dt.uint8
FP8X4 = mybir.dt.float8_e4m3fn_x4
FP4X4 = mybir.dt.float4_e2m1fn_x4
ACT = mybir.ActivationFunctionType
ALU = mybir.AluOpType

P = 128
PACK = 4
PASS = P * PACK
GROUPS = D // PASS
RUN = 8
BLOCKS = P // RUN
QUADRANTS, SCALE_ROWS = 4, 4
TOK_TILES = TOKENS // P
UNITS = HEADS * GROUPS
STEPS = UNITS * PACK
BANKS = 4
GAIN_ROW = 64
LN_LOW, LN_HIGH = 2.0**-63, 2.0**64
SCALAR_BANKS = 10
HIDDEN_LEAD = 5


def tile_draft_heads_shared_unembedding_k7_kernel(
    tc, x, w_words, w_scales, branch_gain, unembed, token_weight, out_0, out_1, out_2
):
    nc = tc.nc
    with ExitStack() as ctx:
        keep = ctx.enter_context(tc.tile_pool(name="keep", bufs=1))
        psum = ctx.enter_context(tc.psum_pool(name="psum", bufs=BANKS))
        ctx.enter_context(tc.manual_schedule())

        with tc.tile_pool(name="early", bufs=1) as early:
            ident32 = keep.tile([P, P], F32, name="ident32")
            ident16 = keep.tile([P, P], BF16, name="ident16")
            gain = keep.tile([P, PACK, UNITS], F32, name="gain")
            ln_w = keep.tile([P, PACK, UNITS], F32, name="ln_w")
            x_res = keep.tile([P, GROUPS, PACK, TOKENS], BF16, name="x_res")
            x_codes = keep.tile([P, GROUPS, TOKENS], U32, name="x_codes", align_bytes=64)
            x_scale = keep.tile([P, GROUPS, TOKENS], U8, name="x_scale", align_bytes=64)
            w_codes = keep.tile([P, HEADS, GROUPS, 2 * D], U8, name="w_codes", align_bytes=64)
            w_scale = keep.tile([P, HEADS, GROUPS, D], U8, name="w_scale", align_bytes=64)
            u_codes = keep.tile([P, GROUPS, VOCAB], U32, name="u_codes", align_bytes=64)
            u_scale = keep.tile([P, GROUPS, VOCAB], U8, name="u_scale", align_bytes=64)

            vec = early.tile([P, PASS], BF16, name="vec")
            vec_sorted = early.tile([P, PACK, P], BF16, name="vec_sorted")
            w_parts = early.tile([P, 2, PACK, UNITS], F32, name="w_parts")
            w_inverse = early.tile([P, PACK, UNITS], F32, name="w_inverse")
            ln_parts = early.tile([P, 2, PACK, UNITS], F32, name="ln_parts")
            x_raw = early.tile([P, TOK_TILES, D], BF16, name="x_raw")
            x_words = early.tile([P, GROUPS, TOK_TILES, 2, P], F32, name="x_words")
            x_sorted = early.tile([P, TOK_TILES, D], BF16, name="x_sorted")
            x_packed = early.tile([P, GROUPS, TOKENS, PACK], BF16, name="x_packed", align_bytes=64)
            w_codes_raw = early.tile([P, HEADS, GROUPS, 2 * D], U8, name="w_codes_raw")
            w_scale_raw = early.tile([P, HEADS * GROUPS, D], U8, name="w_scale_raw")
            u_raw = early.tile([P, GROUPS, PACK, VOCAB], BF16, name="u_raw")


            def load_x(g, pair):
                toks = slice(2 * pair * P, 2 * (pair + 1) * P)
                feats = slice(g * PASS, (g + 1) * PASS)
                nc.sync.dma_start(
                    out=x_raw[:, 2 * pair : 2 * pair + 2, feats], in_=x[toks, feats].rearrange("(c p) d -> p c d", p=P)
                )

            def load_w(h):
                nc.sync.dma_start(
                    out=w_codes_raw[:, h, :, :].bitcast(I32),
                    in_=w_words[GROUPS * h : GROUPS * (h + 1), :, :].rearrange("a p n -> p a n").bitcast(I32),
                )

            def load_w_scale(first, stop):
                passes = slice(GROUPS * first, GROUPS * stop)
                nc.vector.memset(w_scale_raw[:, passes, :].rearrange("p a n -> p (a n)").bitcast(I32), 0)
                for quad in range(QUADRANTS):
                    rows = slice(SCALE_ROWS * quad, SCALE_ROWS * (quad + 1))
                    nc.sync.dma_start(
                        out=w_scale_raw[32 * quad : 32 * quad + SCALE_ROWS, passes, :].bitcast(I32),
                        in_=w_scales[passes, rows, :].rearrange("a r n -> r a n").bitcast(I32),
                    )

            def load_u(kg):
                rows = unembed[kg * PASS : (kg + 1) * PASS, :].rearrange("(q t r) v -> t q r v", t=PACK, r=RUN)
                for t in range(PACK):
                    nc.sync.dma_start(out=u_raw[:, kg, t, :], in_=rows[t])

            nc.gpsimd.memset(vec[:].bitcast(I32), 0)
            make_identity(nc, ident16[:])
            make_identity(nc, ident32[:])
            nc.sync.dma_start(out=vec[0:UNITS, :], in_=token_weight.rearrange("h (g v) -> (h g) v", g=GROUPS))
            nc.sync.dma_start(
                out=vec[GAIN_ROW : GAIN_ROW + UNITS, :], in_=branch_gain.rearrange("h (g v) -> (h g) v", g=GROUPS)
            )
            for g in range(GROUPS):
                for pair in range(TOK_TILES // 2):
                    load_x(g, pair)
            load_w(0)
            load_w_scale(0, 1)
            load_u(0)
            load_w(1)
            load_w_scale(1, 2)
            load_u(1)
            load_w(2)
            load_w_scale(2, HEADS)
            load_w(3)


            x_packed_pairs = (
                x_packed[:].rearrange("p g n t -> p (g n t)").bitcast(F32).rearrange("p (g n half) -> p g n half", g=GROUPS, half=2)
            )
            pair_banks = {}

            def transpose_x_pairs(g, pair):
                tiles = slice(2 * pair, 2 * pair + 2)
                nc.vector.tensor_copy(
                    out=x_words[:, g, tiles, :, :],
                    in_=x_raw[:, tiles, g * PASS : (g + 1) * PASS].bitcast(F32).rearrange("a c (p half) -> a c half p", half=2),
                )
                pair_banks[g, pair] = psum.tile([P, 2, 2, P], F32, name="x_words_t", tag="mm")
                for c in range(2):
                    for half in range(2):
                        nc.tensor.transpose(
                            pair_banks[g, pair][:, c, half, :], x_words[:, g, 2 * pair + c, half, :], ident32[:]
                        )

            def pack_x(g, pair):
                toks = slice(2 * pair * P, 2 * (pair + 1) * P)
                nc.scalar.copy(
                    out=x_packed_pairs[:, g, toks, :].rearrange("p (c n) half -> p c n half", c=2),
                    in_=pair_banks[g, pair][:].rearrange("p c half n -> p c n half"),
                )

            def quantize_x(g):
                nc.vector.quantize_mx(
                    out=x_codes[:, g, :].bitcast(FP8X4),
                    scales=x_scale[:, g, :],
                    in_=x_packed[:, g, :, :].rearrange("p n t -> p (n t)"),
                )


            def sort_runs(dst, src, run_words):
                nc.vector.tensor_copy(
                    out=dst.rearrange("p (b t q w) -> p b t q w", t=PACK, q=BLOCKS, w=run_words),
                    in_=src.rearrange("p (b q t w) -> p b t q w", t=PACK, q=BLOCKS, w=run_words),
                )

            def sort_w_codes(h):
                sort_runs(
                    w_codes[:, h, :, :].rearrange("p a n -> p (a n)").bitcast(I32),
                    w_codes_raw[:, h, :, :].rearrange("p a n -> p (a n)").bitcast(I32),
                    RUN * 2 // 4,
                )

            def sort_w_scale(h):
                sort_runs(
                    w_scale[:, h, :, :].rearrange("p a n -> p (a n)").bitcast(I32),
                    w_scale_raw[:, GROUPS * h : GROUPS * (h + 1), :].rearrange("p a n -> p (a n)").bitcast(I32),
                    RUN // 4,
                )

            def sort_w(h):
                sort_w_codes(h)
                sort_w_scale(h)

            def sort_x(g):
                feats = slice(g * PASS, (g + 1) * PASS)
                nc.vector.tensor_copy(
                    out=x_sorted[:, :, feats].bitcast(F32).rearrange("a c (t q w) -> a c t q w", t=PACK, q=BLOCKS),
                    in_=x_raw[:, :, feats].bitcast(F32).rearrange("a c (q t w) -> a c t q w", t=PACK, q=BLOCKS),
                )

            def transpose_x_residual(g):
                for first in range(0, PACK, 2):
                    bank = psum.tile([P, 2, TOKENS], BF16, name="x_res_t", tag="tr")
                    for t in range(first, first + 2):
                        col = g * PASS + t * P
                        for c in range(TOK_TILES):
                            nc.tensor.transpose(
                                bank[:, t - first, c * P : (c + 1) * P], x_sorted[:, c, col : col + P], ident16[:]
                            )
                    nc.scalar.copy(out=x_res[:, g, first : first + 2, :], in_=bank[:])


            silu, hidden, hidden_packed, h_codes, h_scale = {}, {}, {}, {}, {}

            def project(u):
                h, g = divmod(u, GROUPS)
                silu[u] = keep.tile([P, PACK, TOKENS], F32, name="silu", tag="silu", bufs=UNITS - 2)
                for t in range(PACK):
                    col = g * PASS + t * P
                    bank = psum.tile([P, TOKENS], F32, name="z", tag="mm")
                    for kg in range(GROUPS):
                        nc.tensor.matmul_mx(
                            out=bank[:],
                            lhsT=w_codes[:, h, kg, 2 * col : 2 * (col + P)].bitcast(FP4X4),
                            lhsT_scale=w_scale[:, h, kg, col : col + P],
                            rhs=x_codes[:, kg, :].bitcast(FP8X4),
                            rhs_scale=x_scale[:, kg, :],
                            start=(kg == 0),
                            stop=(kg == GROUPS - 1),
                        )
                    nc.scalar.activation(out=silu[u][:, t, :], in_=bank[:], func=ACT.Silu)

            def residual(u):
                hidden[u] = keep.tile([P, PACK, TOKENS], BF16, name="hidden", tag="hidden", bufs=2)
                for t in range(PACK):
                    nc.vector.scalar_tensor_tensor(
                        out=hidden[u][:, t, :],
                        in0=silu[u][:, t, :],
                        scalar=gain[:, t, u : u + 1],
                        in1=x_res[:, u % GROUPS, t, :],
                        op0=ALU.mult,
                        op1=ALU.add,
                    )

            def interleave(dst, src):
                nc.vector.tensor_copy(
                    out=dst.rearrange("p (c i) t -> p c t i", i=4), in_=src.rearrange("p t (c i) -> p c t i", i=4)
                )

            def pack_hidden(u):
                hidden_packed[u] = keep.tile(
                    [P, TOKENS, PACK], BF16, name="hidden_packed", tag="hidden_packed", bufs=2, align_bytes=64
                )
                interleave(hidden_packed[u][:], hidden[u][:])

            def quantize_hidden(u):
                h_codes[u] = keep.tile([P, TOKENS], U32, name="h_codes", tag="h_codes", bufs=6, align_bytes=64)
                h_scale[u] = keep.tile([P, TOKENS], U8, name="h_scale", tag="h_scale", bufs=6, align_bytes=64)
                nc.vector.quantize_mx(
                    out=h_codes[u][:].bitcast(FP8X4),
                    scales=h_scale[u][:],
                    in_=hidden_packed[u][:].rearrange("p n t -> p (n t)"),
                )

            u_packed = {}

            def pack_u(kg, g):
                u_packed[kg, g] = early.tile(
                    [P, PACK, P, PACK], BF16, name="u_packed", tag="u_packed", bufs=2, align_bytes=64
                )
                nc.vector.tensor_copy(
                    out=u_packed[kg, g][:].rearrange("p t m j -> p m t j"),
                    in_=u_raw[:, kg, :, g * PASS : (g + 1) * PASS].rearrange("p j (m t) -> p m t j", t=PACK),
                )

            def quantize_u(kg, g):
                nc.vector.quantize_mx(
                    out=u_codes[:, kg, g * PASS : (g + 1) * PASS].bitcast(FP8X4),
                    scales=u_scale[:, kg, g * PASS : (g + 1) * PASS],
                    in_=u_packed[kg, g][:].rearrange("p t m j -> p (t m j)"),
                )

            nc.vector.tensor_copy(
                out=vec_sorted[0:GAIN_ROW, :, :], in_=vec[0:GAIN_ROW, :].rearrange("a (p t) -> a t p", t=PACK)
            )
            nc.vector.tensor_copy(
                out=vec_sorted[GAIN_ROW:P, :, :].rearrange("a t (q r) -> a t q r", r=RUN),
                in_=vec[GAIN_ROW:P, :].rearrange("a (q t r) -> a t q r", t=PACK, r=RUN),
            )
            vec_t = psum.tile([P, PACK, P], BF16, name="vec_t", tag="tr")
            for t in range(PACK):
                nc.tensor.transpose(vec_t[:, t, :], vec_sorted[:, t, :], ident16[:])
            weight = vec_t[:, :, 0:UNITS]

            transpose_x_pairs(0, 0)
            nc.vector.tensor_scalar(
                out=w_parts[:, 0, :, :], in0=weight, scalar1=LN_LOW, scalar2=LN_HIGH, op0=ALU.max, op1=ALU.min
            )
            transpose_x_pairs(0, 1)
            nc.vector.reciprocal(out=w_inverse[:], in_=w_parts[:, 0, :, :])
            transpose_x_pairs(1, 0)
            nc.vector.tensor_tensor(out=w_parts[:, 1, :, :], in0=weight, in1=w_inverse[:], op=ALU.mult)
            nc.scalar.activation(out=ln_parts[:], in_=w_parts[:], func=ACT.Ln)
            transpose_x_pairs(1, 1)
            sort_x(0)
            for g in range(GROUPS):
                for pair in range(TOK_TILES // 2):
                    pack_x(g, pair)
            sort_w_codes(0)
            quantize_x(0)
            nc.vector.tensor_copy(out=gain[:], in_=vec_t[:, :, GAIN_ROW : GAIN_ROW + UNITS])
            sort_w_scale(0)
            quantize_x(1)
            sort_x(1)
            for g in range(GROUPS):
                project(g)
                transpose_x_residual(g)
            nc.vector.tensor_tensor(out=ln_w[:], in0=ln_parts[:, 0, :, :], in1=ln_parts[:, 1, :, :], op=ALU.add)

            pack_u(0, 0)
            pack_u(0, 1)
            quantize_u(0, 0)
            sort_w(1)
            quantize_u(0, 1)
            project(2)
            project(3)
            residual(0)
            pack_u(1, 0)
            pack_hidden(0)
            sort_w(2)
            project(4)
            project(5)
            quantize_u(1, 0)
            residual(1)
            quantize_hidden(0)
            sort_w(3)
            project(6)
            project(7)
            pack_hidden(1)
            pack_u(1, 1)
            quantize_hidden(1)
            residual(2)
            quantize_u(1, 1)


        late = ctx.enter_context(tc.tile_pool(name="late", bufs=1))
        y_scale = late.tile([P, GROUPS, HEADS * TOKENS], U8, name="y_scale", align_bytes=64)
        y_t, y_packed, y_banks, y_rows, y_codes, logits = {}, {}, {}, {}, {}, {}
        last = UNITS - 1
        every, first_half, second_half = slice(0, TOKENS), slice(0, TOKENS // 2), slice(TOKENS // 2, TOKENS)

        def unembed_matmuls(i):
            u, t = divmod(i, PACK)
            h, g = divmod(u, GROUPS)
            col = g * PASS + t * P
            logits[i] = psum.tile([P, TOKENS], F32, name="logits", tag="mm")
            for kg in range(GROUPS):
                nc.tensor.matmul_mx(
                    out=logits[i][:],
                    lhsT=u_codes[:, kg, col : col + P].bitcast(FP8X4),
                    lhsT_scale=u_scale[:, kg, col : col + P],
                    rhs=h_codes[GROUPS * h + kg][:].bitcast(FP8X4),
                    rhs_scale=h_scale[GROUPS * h + kg][:],
                    start=(kg == 0),
                    stop=(kg == GROUPS - 1),
                )

        def soft_cap(i):
            u, t = divmod(i, PACK)
            if t == 0:
                y_t[u] = keep.tile([P, PACK, TOKENS], F32, name="y_t", tag="y_t", bufs=3)
            nc.scalar.activation(out=y_t[u][:, t, :], in_=logits[i][:], func=ACT.Tanh)

        def weigh(i, toks):
            u, t = divmod(i, PACK)
            nc.scalar.activation(
                out=y_t[u][:, t, toks], in_=y_t[u][:, t, toks], func=ACT.Exp, bias=ln_w[:, t, u : u + 1], scale=CAP
            )

        def transpose_y(u, c):
            if c == 0:
                y_rows[u] = late.tile([P, TOK_TILES, PASS], F32, name="y_rows", tag="y_rows", bufs=3)
            y_banks[u, c] = psum.tile([P, PACK, P], F32, name="y_bank", tag="tr")
            for t in range(PACK):
                nc.tensor.transpose(y_banks[u, c][:, t, :], y_t[u][:, t, c * P : (c + 1) * P], ident32[:])

        def store_rows(u, c, copy):
            h, g = divmod(u, GROUPS)
            copy(
                out=y_rows[u][:, c, :].rearrange("a (p t) -> a p t", t=PACK),
                in_=y_banks[u, c][:].rearrange("a t p -> a p t"),
            )
            dest = out_0[h, :, g * PASS : (g + 1) * PASS].rearrange("(c p) v -> p c v", p=P)
            nc.sync.dma_start(out=dest[:, c, :], in_=y_rows[u][:, c, :])

        def pack_y(u, toks):
            if toks.start == 0:
                y_packed[u] = late.tile(
                    [P, TOKENS, PACK], BF16, name="y_packed", tag="y_packed", bufs=2, align_bytes=64
                )
            interleave(y_packed[u][:, toks, :], y_t[u][:, :, toks])

        def quantize_y(u, toks):
            h, g = divmod(u, GROUPS)
            y_codes[u, toks.start] = late.tile(
                [P, toks.stop - toks.start], U32, name="y_codes", tag="y_codes", bufs=4, align_bytes=64
            )
            nc.vector.quantize_mx(
                out=y_codes[u, toks.start][:].bitcast(FP8X4),
                scales=y_scale[:, g, h * TOKENS + toks.start : h * TOKENS + toks.stop],
                in_=y_packed[u][:, toks, :].rearrange("p n t -> p (n t)"),
            )

        def store_codes(u, toks):
            h, g = divmod(u, GROUPS)
            code_bytes = slice(PACK * (h * TOKENS + toks.start), PACK * (h * TOKENS + toks.stop))
            nc.sync.dma_start(
                out=out_1[g].rearrange("p m t -> p (m t)")[:, code_bytes].bitcast(I32),
                in_=y_codes[u, toks.start][:].bitcast(I32),
            )

        def store_scales(first, stop):
            cols = slice(first * TOKENS, stop * TOKENS)
            for quad in range(QUADRANTS):
                rows = slice(SCALE_ROWS * quad, SCALE_ROWS * (quad + 1))
                nc.sync.dma_start(
                    out=out_2[:, rows, cols].rearrange("g r m -> r g m").bitcast(I32),
                    in_=y_scale[32 * quad : 32 * quad + SCALE_ROWS, :, cols].bitcast(I32),
                )

        def vector_round(u):
            ahead = u + HIDDEN_LEAD
            if u < last - 1:
                pack_y(u, every)
            if ahead - 1 < UNITS:
                quantize_hidden(ahead - 1)
            if ahead < UNITS:
                residual(ahead)
            for c in range(TOK_TILES):
                if TOK_TILES * u + c >= SCALAR_BANKS:
                    store_rows(u, c, nc.vector.tensor_copy)
            if u == last - 1:
                pack_y(u, every)
            else:
                quantize_y(u, every)
            if ahead < UNITS:
                pack_hidden(ahead)

        for i in range(BANKS):
            unembed_matmuls(i)
        soft_cap(0)
        unembed_matmuls(BANKS)
        for u in range(2, HIDDEN_LEAD - 1):
            pack_hidden(u)
            residual(u + 1)
            quantize_hidden(u)
        pack_hidden(HIDDEN_LEAD - 1)

        head1 = GROUPS * PACK
        deferred = (head1, head1 + 1)
        scale_batches = {3: (0, 2), 5: (2, 3)}
        for i in range(STEPS - PACK):
            u, t = divmod(i, PACK)
            soft_cap(i + 1)
            refill = i + 1 + BANKS
            if refill < STEPS and refill not in deferred:
                unembed_matmuls(refill)
            weigh(i, every)
            if t == PACK - 1:
                transpose_y(u, 0)
                transpose_y(u, 1)
            if t == 0 and u > 0:
                transpose_y(u - 1, 2)
                transpose_y(u - 1, 3)
                if u == 1:
                    for step in deferred:
                        unembed_matmuls(step)
                vector_round(u - 1)
            if 0 <= i - PACK < SCALAR_BANKS:
                store_rows(u - 1, t, nc.scalar.copy)
            if t == PACK - 1 and u > 0:
                store_codes(u - 1, every)
                if u - 1 in scale_batches:
                    store_scales(*scale_batches[u - 1])

        soft_cap(STEPS - 3)
        transpose_y(last - 1, 2)
        transpose_y(last - 1, 3)
        vector_round(last - 1)
        soft_cap(STEPS - 2)
        soft_cap(STEPS - 1)
        for c in range(TOK_TILES):
            for t in range(PACK):
                weigh(STEPS - PACK + t, slice(c * P, (c + 1) * P))
            transpose_y(last, c)
            if c > 0:
                store_rows(last, c - 1, nc.scalar.copy)
            if c == TOK_TILES - 2:
                pack_y(last, first_half)
                quantize_y(last - 1, every)
                store_codes(last - 1, every)
        quantize_y(last, first_half)
        store_codes(last, first_half)
        pack_y(last, second_half)
        store_rows(last, TOK_TILES - 1, nc.scalar.copy)
        quantize_y(last, second_half)
        store_codes(last, second_half)
        store_scales(HEADS - 1, HEADS)
